import numpy as np
import ml_dtypes


def mxq(x, axis, fmt="e4m3"):
    dtype, down = {"e4m3": (ml_dtypes.float8_e4m3fn, 7), "e5m2": (ml_dtypes.float8_e5m2, 14)}[fmt]
    v = np.moveaxis(np.asarray(x, np.float32).astype(ml_dtypes.bfloat16).astype(np.float64), axis, -1)
    blocks = v.reshape(v.shape[:-1] + (-1, 32))
    amax = np.abs(blocks).max(-1, keepdims=True)
    byte = np.maximum(np.where(amax > 0, np.frexp(amax)[1] - 1 + 127, 0) - down, 1)
    scale = np.exp2(byte - 127.0)
    codes = (blocks / scale).astype(np.float32).astype(dtype).astype(np.float64)
    return np.moveaxis((codes * scale).reshape(v.shape), -1, axis)


WIDE = False


def mx_kscale(k, group=512):
    if not WIDE:
        return np.ones(k)
    levels = np.array([18, -18])
    if group != 512:
        return np.exp2(np.random.permutation(np.resize(levels, k // group))).repeat(group)
    if k % 512:
        return np.exp2(np.random.permutation(np.resize(levels, k // 32))).repeat(32)
    a = np.empty((k // 512, 16))
    for p in range(k // 512):
        a[p, :8] = np.random.permutation(np.resize(levels, 8))
        for g in range(8):
            far = levels[np.abs(levels - a[p, g]) >= 10]
            a[p, g + 8] = far[np.random.randint(len(far))]
    return np.exp2(a.ravel()).repeat(32)


def f64(x):
    return np.asarray(x).astype(np.float64)


G, D, J, K, L = 8, 128, 128, 128, 128


def setup_inputs():
    n = np.random.standard_normal
    s_d = mx_kscale(D, 0)
    s_j = mx_kscale(J, 0)
    return {
        "x": (n((G, D, J)) * s_d[:, None] * s_j).astype(np.float32),
        "a": (n((D, K)) / np.sqrt(D) / s_d[:, None]).astype(np.float32),
        "b": (n((J, L)) / np.sqrt(J) / s_j[:, None]).astype(np.float32),
        "cw": (np.random.uniform(0.5, 2.0, (K, L))).astype(np.float32),
    }


def reference(x, a, b, cw):
    xq = mxq(f64(x), 1, "e4m3")
    aq = mxq(f64(a), 0, "e4m3")
    z = xq.transpose(0, 2, 1) @ aq
    zq = mxq(z, 1, "e4m3")
    bq = mxq(f64(b), 0, "e4m3")
    w = zq.transpose(0, 2, 1) @ bq
    y = w * f64(cw)
    return y

@@ -1,0 +1,130 @@
+from contextlib import ExitStack
+
+import concourse.mybir as mybir
+
+G, D, J, K, L = 8, 128, 128, 128, 128
+FLOPS = 2 * G * (D * J * K + J * K * L)
+
+F32 = mybir.dt.float32
+BF16 = mybir.dt.bfloat16
+U32 = mybir.dt.uint32
+U8 = mybir.dt.uint8
+FP8X4 = mybir.dt.float8_e4m3fn_x4
+
+P = 128
+R = 32
+PACK = 4
+SETS = 2
+TILES = 4
+W = 128
+
+
+def tile_rows_kron_sep_kernel(tc, x, a, b, cw, out):
+    nc = tc.nc
+    with ExitStack() as ctx:
+        sb = ctx.enter_context(tc.tile_pool(name="sb", bufs=1))
+        ps = ctx.enter_context(tc.psum_pool(name="ps", bufs=1))
+        ctx.enter_context(tc.manual_schedule())
+
+        top = R + SETS * R
+        raw = sb.tile([top, TILES + 1, PACK, W], F32, name="raw", align_bytes=64)
+        b_raw = sb.tile([P, PACK, W], F32, name="b_raw", align_bytes=64)
+        cw_sb = sb.tile([P, 2, L], F32, name="cw_sb", align_bytes=64)
+        x_bf = sb.tile([top, PACK, TILES, R, PACK], BF16, name="x_bf", align_bytes=64)
+        a_bf = sb.tile([top, K, PACK], BF16, name="a_bf", align_bytes=64)
+        b_bf = sb.tile([P, L, PACK], BF16, name="b_bf", align_bytes=64)
+        z_bf = sb.tile([P, 2, SETS, K // 2, PACK], BF16, name="z_bf", align_bytes=64)
+        x_codes = sb.tile([top, PACK, W], U32, name="x_codes", align_bytes=64)
+        x_scales = sb.tile([top, PACK, W], U8, name="x_scales", align_bytes=64)
+        a_codes = sb.tile([top, W], U32, name="a_codes", align_bytes=64)
+        a_scales = sb.tile([top, W], U8, name="a_scales", align_bytes=64)
+        b_codes = sb.tile([P, W], U32, name="b_codes", align_bytes=64)
+        b_scales = sb.tile([P, W], U8, name="b_scales", align_bytes=64)
+        z_codes = sb.tile([P, 2, W], U32, name="z_codes", align_bytes=64)
+        z_scales = sb.tile([P, 2, W], U8, name="z_scales", align_bytes=64)
+        res = sb.tile([P, TILES, 2, L], F32, name="res", align_bytes=64)
+        z_ps = [ps.tile([P, PACK, K], F32, name="z_ps%d" % s) for s in range(SETS)]
+        w_ps = [ps.tile([P, 2, L], F32, name="w_ps%d" % c) for c in range(TILES)]
+
+        a_rows = a.rearrange("(p u) k -> p u k", u=PACK)
+        b_rows = b.rearrange("(p t) l -> p t l", t=PACK)
+        cw_rows = cw.rearrange("(q h) l -> q h l", h=2)
+
+        def load_x(c):
+            nc.sync.dma_start(
+                out=raw[R:top, c],
+                in_=x[SETS * c : SETS * (c + 1)].rearrange("s (p u) j -> (s p) u j", u=PACK),
+            )
+
+        load_x(0)
+        for s in range(SETS):
+            nc.scalar.dma_start(out=raw[R * (s + 1) : R * (s + 2), TILES], in_=a_rows)
+        for c in range(1, TILES):
+            load_x(c)
+        for c in (0, 2, 1, 3):
+            nc.sync.dma_start(out=b_raw[R * c : R * (c + 1)], in_=b_rows)
+        for s in range(SETS):
+            nc.sync.dma_start(out=cw_sb[64 * s : 64 * (s + 1)], in_=cw_rows)
+
+        nc.vector.memset(raw[0:R].rearrange("p c u j -> p (c u j)"), 0.0)
+
+        def deal_x(copy, c, t0, t1):
+            copy(
+                out=x_bf[:, t0:t1, c],
+                in_=raw[:, c].rearrange("p u (m t) -> p t m u", t=PACK)[:, t0:t1],
+            )
+
+        def quantise(codes, scales, values):
+            nc.vector.quantize_mx(out=codes.bitcast(FP8X4), scales=scales, in_=values)
+
+        vcopy = nc.vector.tensor_copy
+        scopy = nc.scalar.copy
+
+        deal_x(scopy, 0, 0, 4)
+        vcopy(out=a_bf[:], in_=raw[:, TILES].rearrange("p u k -> p k u"))
+        deal_x(vcopy, 1, 0, 2)
+        deal_x(scopy, 1, 2, 4)
+        quantise(a_codes[:], a_scales[:], a_bf[:].rearrange("p k u -> p (k u)"))
+        deal_x(vcopy, 2, 0, 4)
+        deal_x(scopy, 3, 2, 4)
+        deal_x(vcopy, 3, 0, 2)
+
+        for t in (2, 3, 0, 1):
+            quantise(x_codes[:, t], x_scales[:, t], x_bf[:, t].rearrange("p c m u -> p (c m u)"))
+            for s in range(SETS):
+                rows = slice(R * (s + 1), R * (s + 2))
+                nc.tensor.matmul_mx(
+                    out=z_ps[s][:, t],
+                    lhsT=x_codes[rows, t].bitcast(FP8X4),
+                    lhsT_scale=x_scales[rows, t],
+                    rhs=a_codes[rows].bitcast(FP8X4),
+                    rhs_scale=a_scales[rows],
+                    start=True,
+                    stop=True,
+                )
+
+        vcopy(out=b_bf[:], in_=b_raw[:].rearrange("p t l -> p l t"))
+        vcopy(out=z_bf[:, :, 0], in_=z_ps[0][:].rearrange("p t (q h) -> p h q t", h=2))
+        scopy(out=z_bf[:, :, 1], in_=z_ps[1][:].rearrange("p t (q h) -> p h q t", h=2))
+        quantise(b_codes[:], b_scales[:], b_bf[:].rearrange("p l t -> p (l t)"))
+
+        for h in range(2):
+            quantise(z_codes[:, h], z_scales[:, h], z_bf[:, h].rearrange("p s q t -> p (s q t)"))
+            for c in range(TILES):
+                rows = slice(R * c, R * (c + 1))
+                nc.tensor.matmul_mx(
+                    out=w_ps[c][:, h],
+                    lhsT=z_codes[rows, h].bitcast(FP8X4),
+                    lhsT_scale=z_scales[rows, h],
+                    rhs=b_codes[rows].bitcast(FP8X4),
+                    rhs_scale=b_scales[rows],
+                    start=True,
+                    stop=True,
+                )
+
+        for c in range(TILES):
+            nc.vector.tensor_tensor(out=res[:, c], in0=w_ps[c][:], in1=cw_sb[:], op=mybir.AluOpType.mult)
+            nc.sync.dma_start(
+                out=out[SETS * c : SETS * (c + 1)].rearrange("s (q h) l -> (s q) h l", h=2),
+                in_=res[:, c],
+            )

@@ -17,6 +17,8 @@ PACK = 4
 SETS = 2
 TILES = 4
 W = 128
+WARM_HEAD = 26
+WARM_MID = 8
 
 
 def tile_rows_kron_sep_kernel(tc, x, a, b, cw, out):
@@ -56,6 +58,8 @@ def tile_rows_kron_sep_kernel(tc, x, a, b, cw, out):
                 in_=x[SETS * c : SETS * (c + 1)].rearrange("s (p u) j -> (s p) u j", u=PACK),
             )
 
+        warm = sb.tile([P, 2, 8], F32, name="warm")
+        nc.gpsimd.memset(warm[:, 0], 0.0)
         load_x(0)
         for s in range(SETS):
             nc.scalar.dma_start(out=raw[R * (s + 1) : R * (s + 2), TILES], in_=a_rows)
@@ -66,12 +70,41 @@ def tile_rows_kron_sep_kernel(tc, x, a, b, cw, out):
         for s in range(SETS):
             nc.sync.dma_start(out=cw_sb[64 * s : 64 * (s + 1)], in_=cw_rows)
 
-        nc.vector.memset(raw[0:R].rearrange("p c u j -> p (c u j)"), 0.0)
+        nc.scalar.copy(out=warm[:, 1], in_=warm[:, 0])
+        zero_bf = sb.tile([P, W * PACK], BF16, name="zero_bf", align_bytes=64)
+        zero_codes = sb.tile([P, W], U32, name="zero_codes", align_bytes=64)
+        zero_scales = sb.tile([P, W], U8, name="zero_scales", align_bytes=64)
+        warm_ps = ps.tile([P, W], F32, name="warm_ps")
+        nc.vector.memset(zero_bf[:], 0.0)
+        nc.vector.memset(raw[0:R, 4].rearrange("p u j -> p (u j)"), 0.0)
+        nc.vector.quantize_mx(out=zero_codes[:].bitcast(FP8X4), scales=zero_scales[:], in_=zero_bf[:])
+        nc.vector.memset(raw[0:R, 0:2].rearrange("p c u j -> p (c u j)"), 0.0)
 
-        def deal_x(copy, c, t0, t1):
+        def keep_warm(n):
+            for i in range(n):
+                nc.tensor.matmul_mx(
+                    out=warm_ps[:],
+                    lhsT=zero_codes[:].bitcast(FP8X4),
+                    lhsT_scale=zero_scales[:],
+                    rhs=zero_codes[:].bitcast(FP8X4),
+                    rhs_scale=zero_scales[:],
+                    start=True,
+                    stop=True,
+                )
+
+        keep_warm(WARM_HEAD)
+        nc.gpsimd.memset(raw[0:R, 2:4].rearrange("p c u j -> p (c u j)"), 0.0)
+
+        def deal_x(copy, c, m0, m1):
             copy(
-                out=x_bf[:, t0:t1, c],
-                in_=raw[:, c].rearrange("p u (m t) -> p t m u", t=PACK)[:, t0:t1],
+                out=x_bf[:, :, c, m0:m1].rearrange("p t m u -> p m u t"),
+                in_=raw[:, c].rearrange("p u (m t) -> p m u t", t=PACK)[:, m0:m1],
+            )
+
+        def interleave(copy, dst, src):
+            copy(
+                out=dst.rearrange("p (n i) u -> p n u i", i=PACK),
+                in_=src.rearrange("p u (n i) -> p n u i", i=PACK),
             )
 
         def quantise(codes, scales, values):
@@ -80,16 +113,16 @@ def tile_rows_kron_sep_kernel(tc, x, a, b, cw, out):
         vcopy = nc.vector.tensor_copy
         scopy = nc.scalar.copy
 
-        deal_x(scopy, 0, 0, 4)
-        vcopy(out=a_bf[:], in_=raw[:, TILES].rearrange("p u k -> p k u"))
-        deal_x(vcopy, 1, 0, 2)
-        deal_x(scopy, 1, 2, 4)
+        deal_x(scopy, 0, 0, R)
+        interleave(vcopy, a_bf[:], raw[:, TILES])
+        deal_x(vcopy, 1, 0, R)
+        deal_x(scopy, 2, 0, 12)
+        deal_x(vcopy, 2, 12, R)
+        deal_x(scopy, 3, 0, 12)
+        deal_x(vcopy, 3, 12, R)
         quantise(a_codes[:], a_scales[:], a_bf[:].rearrange("p k u -> p (k u)"))
-        deal_x(vcopy, 2, 0, 4)
-        deal_x(scopy, 3, 2, 4)
-        deal_x(vcopy, 3, 0, 2)
 
-        for t in (2, 3, 0, 1):
+        for t in range(PACK):
             quantise(x_codes[:, t], x_scales[:, t], x_bf[:, t].rearrange("p c m u -> p (c m u)"))
             for s in range(SETS):
                 rows = slice(R * (s + 1), R * (s + 2))
@@ -103,10 +136,12 @@ def tile_rows_kron_sep_kernel(tc, x, a, b, cw, out):
                     stop=True,
                 )
 
-        vcopy(out=b_bf[:], in_=b_raw[:].rearrange("p t l -> p l t"))
-        vcopy(out=z_bf[:, :, 0], in_=z_ps[0][:].rearrange("p t (q h) -> p h q t", h=2))
-        scopy(out=z_bf[:, :, 1], in_=z_ps[1][:].rearrange("p t (q h) -> p h q t", h=2))
+        keep_warm(WARM_MID)
+        interleave(scopy, b_bf[:], b_raw[:])
         quantise(b_codes[:], b_scales[:], b_bf[:].rearrange("p l t -> p (l t)"))
+        for h in range(2):
+            vcopy(out=z_bf[:, h, 0], in_=z_ps[0][:].rearrange("p t (q h) -> p h q t", h=2)[:, h])
+            scopy(out=z_bf[:, h, 1], in_=z_ps[1][:].rearrange("p t (q h) -> p h q t", h=2)[:, h])
 
         for h in range(2):
             quantise(z_codes[:, h], z_scales[:, h], z_bf[:, h].rearrange("p s q t -> p (s q t)"))

@@ -8,6 +8,7 @@ FLOPS = 2 * G * (D * J * K + J * K * L)
 F32 = mybir.dt.float32
 BF16 = mybir.dt.bfloat16
 U32 = mybir.dt.uint32
+I32 = mybir.dt.int32
 U8 = mybir.dt.uint8
 FP8X4 = mybir.dt.float8_e4m3fn_x4
 
@@ -17,8 +18,8 @@ PACK = 4
 SETS = 2
 TILES = 4
 W = 128
-WARM_HEAD = 26
-WARM_MID = 8
+WARM_HEAD = 20
+WARM_MID = 7
 
 
 def tile_rows_kron_sep_kernel(tc, x, a, b, cw, out):
@@ -46,7 +47,13 @@ def tile_rows_kron_sep_kernel(tc, x, a, b, cw, out):
         z_scales = sb.tile([P, 2, W], U8, name="z_scales", align_bytes=64)
         res = sb.tile([P, TILES, 2, L], F32, name="res", align_bytes=64)
         z_ps = [ps.tile([P, PACK, K], F32, name="z_ps%d" % s) for s in range(SETS)]
-        w_ps = [ps.tile([P, 2, L], F32, name="w_ps%d" % c) for c in range(TILES)]
+        w_first = [ps.tile([P, 2, L], F32, name="w_ps%d" % c) for c in range(TILES)]
+        w_extra = ps.tile([P, L], F32, name="w_extra")
+        w_ps = {(c, 0): w_first[c][:, 0] for c in range(TILES)}
+        w_ps[0, 1] = w_extra[:]
+        w_ps[1, 1] = z_ps[0][:, 0]
+        w_ps[2, 1] = z_ps[1][:, 0]
+        w_ps[3, 1] = w_first[3][:, 1]
 
         a_rows = a.rearrange("(p u) k -> p u k", u=PACK)
         b_rows = b.rearrange("(p t) l -> p t l", t=PACK)
@@ -76,9 +83,10 @@ def tile_rows_kron_sep_kernel(tc, x, a, b, cw, out):
         zero_scales = sb.tile([P, W], U8, name="zero_scales", align_bytes=64)
         warm_ps = ps.tile([P, W], F32, name="warm_ps")
         nc.vector.memset(zero_bf[:], 0.0)
-        nc.vector.memset(raw[0:R, 4].rearrange("p u j -> p (u j)"), 0.0)
+        nc.vector.memset(raw[0:R, 4].rearrange("p u j -> p (u j)").bitcast(I32), 0)
         nc.vector.quantize_mx(out=zero_codes[:].bitcast(FP8X4), scales=zero_scales[:], in_=zero_bf[:])
-        nc.vector.memset(raw[0:R, 0:2].rearrange("p c u j -> p (c u j)"), 0.0)
+        nc.vector.memset(raw[0:R, 0:2].rearrange("p c u j -> p (c u j)").bitcast(I32), 0)
+        nc.vector.memset(raw[0:R, 2:4].rearrange("p c u j -> p (c u j)").bitcast(I32), 0)
 
         def keep_warm(n):
             for i in range(n):
@@ -93,7 +101,6 @@ def tile_rows_kron_sep_kernel(tc, x, a, b, cw, out):
                 )
 
         keep_warm(WARM_HEAD)
-        nc.gpsimd.memset(raw[0:R, 2:4].rearrange("p c u j -> p (c u j)"), 0.0)
 
         def deal_x(copy, c, m0, m1):
             copy(
@@ -137,18 +144,25 @@ def tile_rows_kron_sep_kernel(tc, x, a, b, cw, out):
                 )
 
         keep_warm(WARM_MID)
-        interleave(scopy, b_bf[:], b_raw[:])
+        interleave(scopy, b_bf[:, 0:64], b_raw[:, :, 0:64])
+        interleave(vcopy, b_bf[:, 64:128], b_raw[:, :, 64:128])
+
+        def leave_psum(copy, s, h, q0, q1):
+            copy(out=z_bf[:, h, s, q0:q1], in_=z_ps[s][:].rearrange("p t (q h) -> p h q t", h=2)[:, h, q0:q1])
+
+        leave_psum(vcopy, 0, 0, 0, 64)
+        leave_psum(scopy, 1, 0, 0, 64)
+        leave_psum(vcopy, 0, 1, 0, 32)
+        leave_psum(scopy, 1, 1, 0, 64)
+        leave_psum(scopy, 0, 1, 32, 64)
         quantise(b_codes[:], b_scales[:], b_bf[:].rearrange("p l t -> p (l t)"))
-        for h in range(2):
-            vcopy(out=z_bf[:, h, 0], in_=z_ps[0][:].rearrange("p t (q h) -> p h q t", h=2)[:, h])
-            scopy(out=z_bf[:, h, 1], in_=z_ps[1][:].rearrange("p t (q h) -> p h q t", h=2)[:, h])
 
         for h in range(2):
             quantise(z_codes[:, h], z_scales[:, h], z_bf[:, h].rearrange("p s q t -> p (s q t)"))
-            for c in range(TILES):
+            for c in ((0, 1, 2, 3), (0, 3, 1, 2))[h]:
                 rows = slice(R * c, R * (c + 1))
                 nc.tensor.matmul_mx(
-                    out=w_ps[c][:, h],
+                    out=w_ps[c, h],
                     lhsT=z_codes[rows, h].bitcast(FP8X4),
                     lhsT_scale=z_scales[rows, h],
                     rhs=b_codes[rows].bitcast(FP8X4),
@@ -157,9 +171,12 @@ def tile_rows_kron_sep_kernel(tc, x, a, b, cw, out):
                     stop=True,
                 )
 
-        for c in range(TILES):
-            nc.vector.tensor_tensor(out=res[:, c], in0=w_ps[c][:], in1=cw_sb[:], op=mybir.AluOpType.mult)
-            nc.sync.dma_start(
-                out=out[SETS * c : SETS * (c + 1)].rearrange("s (q h) l -> (s q) h l", h=2),
-                in_=res[:, c],
+        steps = [(0, 0, 1), (1, 0, 1), (2, 0, 1), (0, 1, 2), (3, 0, 2), (1, 1, 2), (2, 1, 2)]
+        for i, (c, h0, h1) in enumerate(steps):
+            sums = w_first[c][:] if h1 - h0 == 2 else w_ps[c, h0].unsqueeze(1)
+            nc.vector.tensor_tensor(out=res[:, c, h0:h1], in0=sums, in1=cw_sb[:, h0:h1], op=mybir.AluOpType.mult)
+            queue = nc.sync if i % 2 == 0 else nc.scalar
+            queue.dma_start(
+                out=out[SETS * c : SETS * (c + 1)].rearrange("s (q h) l -> (s q) h l", h=2)[:, h0:h1],
+                in_=res[:, c, h0:h1],
             )

@@ -8,7 +8,6 @@ FLOPS = 2 * G * (D * J * K + J * K * L)
 F32 = mybir.dt.float32
 BF16 = mybir.dt.bfloat16
 U32 = mybir.dt.uint32
-I32 = mybir.dt.int32
 U8 = mybir.dt.uint8
 FP8X4 = mybir.dt.float8_e4m3fn_x4
 
@@ -18,8 +17,9 @@ PACK = 4
 SETS = 2
 TILES = 4
 W = 128
-WARM_HEAD = 20
-WARM_MID = 7
+WARM_HEAD = 17
+WARM_LATE = 7
+WARM_MID = 8
 
 
 def tile_rows_kron_sep_kernel(tc, x, a, b, cw, out):
@@ -34,13 +34,13 @@ def tile_rows_kron_sep_kernel(tc, x, a, b, cw, out):
         b_raw = sb.tile([P, PACK, W], F32, name="b_raw", align_bytes=64)
         cw_sb = sb.tile([P, 2, L], F32, name="cw_sb", align_bytes=64)
         x_bf = sb.tile([top, PACK, TILES, R, PACK], BF16, name="x_bf", align_bytes=64)
-        a_bf = sb.tile([top, K, PACK], BF16, name="a_bf", align_bytes=64)
+        a_bf = sb.tile([P, K, PACK], BF16, name="a_bf", align_bytes=64)
         b_bf = sb.tile([P, L, PACK], BF16, name="b_bf", align_bytes=64)
         z_bf = sb.tile([P, 2, SETS, K // 2, PACK], BF16, name="z_bf", align_bytes=64)
         x_codes = sb.tile([top, PACK, W], U32, name="x_codes", align_bytes=64)
         x_scales = sb.tile([top, PACK, W], U8, name="x_scales", align_bytes=64)
-        a_codes = sb.tile([top, W], U32, name="a_codes", align_bytes=64)
-        a_scales = sb.tile([top, W], U8, name="a_scales", align_bytes=64)
+        a_codes = sb.tile([P, W], U32, name="a_codes", align_bytes=64)
+        a_scales = sb.tile([P, W], U8, name="a_scales", align_bytes=64)
         b_codes = sb.tile([P, W], U32, name="b_codes", align_bytes=64)
         b_scales = sb.tile([P, W], U8, name="b_scales", align_bytes=64)
         z_codes = sb.tile([P, 2, W], U32, name="z_codes", align_bytes=64)
@@ -78,29 +78,38 @@ def tile_rows_kron_sep_kernel(tc, x, a, b, cw, out):
             nc.sync.dma_start(out=cw_sb[64 * s : 64 * (s + 1)], in_=cw_rows)
 
         nc.scalar.copy(out=warm[:, 1], in_=warm[:, 0])
-        zero_bf = sb.tile([P, W * PACK], BF16, name="zero_bf", align_bytes=64)
+        zero = sb.tile([P, W * PACK // 2], F32, name="zero", align_bytes=64)
         zero_codes = sb.tile([P, W], U32, name="zero_codes", align_bytes=64)
         zero_scales = sb.tile([P, W], U8, name="zero_scales", align_bytes=64)
         warm_ps = ps.tile([P, W], F32, name="warm_ps")
-        nc.vector.memset(zero_bf[:], 0.0)
-        nc.vector.memset(raw[0:R, 4].rearrange("p u j -> p (u j)").bitcast(I32), 0)
-        nc.vector.quantize_mx(out=zero_codes[:].bitcast(FP8X4), scales=zero_scales[:], in_=zero_bf[:])
-        nc.vector.memset(raw[0:R, 0:2].rearrange("p c u j -> p (c u j)").bitcast(I32), 0)
-        nc.vector.memset(raw[0:R, 2:4].rearrange("p c u j -> p (c u j)").bitcast(I32), 0)
+        nc.vector.memset(zero[:], 0.0)
+        nc.vector.memset(a_bf[top:P].rearrange("p k u -> p (k u)"), 0.0)
+        nc.vector.quantize_mx(out=zero_codes[:].bitcast(FP8X4), scales=zero_scales[:], in_=zero[:].bitcast(BF16))
 
-        def keep_warm(n):
+        def fill(c0, c1):
+            n = 2 * (c1 - c0)
+            nc.vector.tensor_copy(
+                out=raw[0:R, c0:c1].rearrange("p c (v u) j -> p (c v) (u j)", u=2),
+                in_=zero[0:R].unsqueeze(1).to_broadcast([R, n, W * PACK // 2]),
+            )
+
+        fill(0, 1)
+        fill(4, 5)
+        fill(1, 4)
+
+        def keep_warm(n, codes, scales):
             for i in range(n):
                 nc.tensor.matmul_mx(
                     out=warm_ps[:],
-                    lhsT=zero_codes[:].bitcast(FP8X4),
-                    lhsT_scale=zero_scales[:],
-                    rhs=zero_codes[:].bitcast(FP8X4),
-                    rhs_scale=zero_scales[:],
+                    lhsT=codes[:].bitcast(FP8X4),
+                    lhsT_scale=scales[:],
+                    rhs=codes[:].bitcast(FP8X4),
+                    rhs_scale=scales[:],
                     start=True,
                     stop=True,
                 )
 
-        keep_warm(WARM_HEAD)
+        keep_warm(WARM_HEAD, zero_codes, zero_scales)
 
         def deal_x(copy, c, m0, m1):
             copy(
@@ -121,13 +130,14 @@ def tile_rows_kron_sep_kernel(tc, x, a, b, cw, out):
         scopy = nc.scalar.copy
 
         deal_x(scopy, 0, 0, R)
-        interleave(vcopy, a_bf[:], raw[:, TILES])
+        interleave(vcopy, a_bf[0:top], raw[:, TILES])
         deal_x(vcopy, 1, 0, R)
         deal_x(scopy, 2, 0, 12)
         deal_x(vcopy, 2, 12, R)
+        quantise(a_codes[:], a_scales[:], a_bf[:].rearrange("p k u -> p (k u)"))
+        keep_warm(WARM_LATE, a_codes, a_scales)
         deal_x(scopy, 3, 0, 12)
         deal_x(vcopy, 3, 12, R)
-        quantise(a_codes[:], a_scales[:], a_bf[:].rearrange("p k u -> p (k u)"))
 
         for t in range(PACK):
             quantise(x_codes[:, t], x_scales[:, t], x_bf[:, t].rearrange("p c m u -> p (c m u)"))
@@ -143,7 +153,7 @@ def tile_rows_kron_sep_kernel(tc, x, a, b, cw, out):
                     stop=True,
                 )
 
-        keep_warm(WARM_MID)
+        keep_warm(WARM_MID, zero_codes, zero_scales)
         interleave(scopy, b_bf[:, 0:64], b_raw[:, :, 0:64])
         interleave(vcopy, b_bf[:, 64:128], b_raw[:, :, 64:128])
 
@@ -172,11 +182,11 @@ def tile_rows_kron_sep_kernel(tc, x, a, b, cw, out):
                 )
 
         steps = [(0, 0, 1), (1, 0, 1), (2, 0, 1), (0, 1, 2), (3, 0, 2), (1, 1, 2), (2, 1, 2)]
-        for i, (c, h0, h1) in enumerate(steps):
+        for c, h0, h1 in steps:
             sums = w_first[c][:] if h1 - h0 == 2 else w_ps[c, h0].unsqueeze(1)
             nc.vector.tensor_tensor(out=res[:, c, h0:h1], in0=sums, in1=cw_sb[:, h0:h1], op=mybir.AluOpType.mult)
-            queue = nc.sync if i % 2 == 0 else nc.scalar
-            queue.dma_start(
-                out=out[SETS * c : SETS * (c + 1)].rearrange("s (q h) l -> (s q) h l", h=2)[:, h0:h1],
-                in_=res[:, c, h0:h1],
-            )
+            if h1 == 2:
+                nc.sync.dma_start(
+                    out=out[SETS * c : SETS * (c + 1)].rearrange("s (q h) l -> (s q) h l", h=2),
+                    in_=res[:, c],
+                )

@@ -8,6 +8,7 @@ FLOPS = 2 * G * (D * J * K + J * K * L)
 F32 = mybir.dt.float32
 BF16 = mybir.dt.bfloat16
 U32 = mybir.dt.uint32
+I32 = mybir.dt.int32
 U8 = mybir.dt.uint8
 FP8X4 = mybir.dt.float8_e4m3fn_x4
 
@@ -17,8 +18,8 @@ PACK = 4
 SETS = 2
 TILES = 4
 W = 128
-WARM_HEAD = 17
-WARM_LATE = 7
+WARM_HEAD = 20
+WARM_LATE = 9
 WARM_MID = 8
 
 
@@ -31,18 +32,22 @@ def tile_rows_kron_sep_kernel(tc, x, a, b, cw, out):
 
         top = R + SETS * R
         raw = sb.tile([top, TILES + 1, PACK, W], F32, name="raw", align_bytes=64)
-        b_raw = sb.tile([P, PACK, W], F32, name="b_raw", align_bytes=64)
         cw_sb = sb.tile([P, 2, L], F32, name="cw_sb", align_bytes=64)
         x_bf = sb.tile([top, PACK, TILES, R, PACK], BF16, name="x_bf", align_bytes=64)
         a_bf = sb.tile([P, K, PACK], BF16, name="a_bf", align_bytes=64)
-        b_bf = sb.tile([P, L, PACK], BF16, name="b_bf", align_bytes=64)
         z_bf = sb.tile([P, 2, SETS, K // 2, PACK], BF16, name="z_bf", align_bytes=64)
         x_codes = sb.tile([top, PACK, W], U32, name="x_codes", align_bytes=64)
         x_scales = sb.tile([top, PACK, W], U8, name="x_scales", align_bytes=64)
-        a_codes = sb.tile([P, W], U32, name="a_codes", align_bytes=64)
-        a_scales = sb.tile([P, W], U8, name="a_scales", align_bytes=64)
-        b_codes = sb.tile([P, W], U32, name="b_codes", align_bytes=64)
-        b_scales = sb.tile([P, W], U8, name="b_scales", align_bytes=64)
+        ab_mx = sb.tile([P, W + W // 4], U32, name="ab_mx", align_bytes=64)
+        b_mx = sb.tile([P, W + W // 4], U32, name="b_mx", align_bytes=64)
+
+        def codes_of(tile, rows):
+            return tile[rows, 0:W]
+
+        def scales_of(tile, rows):
+            return tile[rows, W : W + W // 4].bitcast(U8)
+
+        every = slice(0, P)
         z_codes = sb.tile([P, 2, W], U32, name="z_codes", align_bytes=64)
         z_scales = sb.tile([P, 2, W], U8, name="z_scales", align_bytes=64)
         res = sb.tile([P, TILES, 2, L], F32, name="res", align_bytes=64)
@@ -70,10 +75,9 @@ def tile_rows_kron_sep_kernel(tc, x, a, b, cw, out):
         load_x(0)
         for s in range(SETS):
             nc.scalar.dma_start(out=raw[R * (s + 1) : R * (s + 2), TILES], in_=a_rows)
+        nc.sync.dma_start(out=raw[0:R, TILES], in_=b_rows)
         for c in range(1, TILES):
             load_x(c)
-        for c in (0, 2, 1, 3):
-            nc.sync.dma_start(out=b_raw[R * c : R * (c + 1)], in_=b_rows)
         for s in range(SETS):
             nc.sync.dma_start(out=cw_sb[64 * s : 64 * (s + 1)], in_=cw_rows)
 
@@ -94,22 +98,22 @@ def tile_rows_kron_sep_kernel(tc, x, a, b, cw, out):
             )
 
         fill(0, 1)
-        fill(4, 5)
+        nc.vector.memset(ab_mx[:, W : W + W // 4], 0)
         fill(1, 4)
 
         def keep_warm(n, codes, scales):
             for i in range(n):
                 nc.tensor.matmul_mx(
                     out=warm_ps[:],
-                    lhsT=codes[:].bitcast(FP8X4),
-                    lhsT_scale=scales[:],
-                    rhs=codes[:].bitcast(FP8X4),
-                    rhs_scale=scales[:],
+                    lhsT=codes.bitcast(FP8X4),
+                    lhsT_scale=scales,
+                    rhs=codes.bitcast(FP8X4),
+                    rhs_scale=scales,
                     start=True,
                     stop=True,
                 )
 
-        keep_warm(WARM_HEAD, zero_codes, zero_scales)
+        keep_warm(WARM_HEAD, zero_codes[:], zero_scales[:])
 
         def deal_x(copy, c, m0, m1):
             copy(
@@ -132,10 +136,12 @@ def tile_rows_kron_sep_kernel(tc, x, a, b, cw, out):
         deal_x(scopy, 0, 0, R)
         interleave(vcopy, a_bf[0:top], raw[:, TILES])
         deal_x(vcopy, 1, 0, R)
+        quantise(codes_of(ab_mx, every), scales_of(ab_mx, every), a_bf[:].rearrange("p k u -> p (k u)"))
+        for c in range(1, TILES):
+            nc.sync.dma_start(out=b_mx[R * c : R * (c + 1)].bitcast(I32), in_=ab_mx[0:R].bitcast(I32))
+        keep_warm(WARM_LATE, codes_of(ab_mx, every), scales_of(ab_mx, every))
         deal_x(scopy, 2, 0, 12)
         deal_x(vcopy, 2, 12, R)
-        quantise(a_codes[:], a_scales[:], a_bf[:].rearrange("p k u -> p (k u)"))
-        keep_warm(WARM_LATE, a_codes, a_scales)
         deal_x(scopy, 3, 0, 12)
         deal_x(vcopy, 3, 12, R)
 
@@ -147,25 +153,21 @@ def tile_rows_kron_sep_kernel(tc, x, a, b, cw, out):
                     out=z_ps[s][:, t],
                     lhsT=x_codes[rows, t].bitcast(FP8X4),
                     lhsT_scale=x_scales[rows, t],
-                    rhs=a_codes[rows].bitcast(FP8X4),
-                    rhs_scale=a_scales[rows],
+                    rhs=codes_of(ab_mx, rows).bitcast(FP8X4),
+                    rhs_scale=scales_of(ab_mx, rows),
                     start=True,
                     stop=True,
                 )
 
-        keep_warm(WARM_MID, zero_codes, zero_scales)
-        interleave(scopy, b_bf[:, 0:64], b_raw[:, :, 0:64])
-        interleave(vcopy, b_bf[:, 64:128], b_raw[:, :, 64:128])
+        keep_warm(WARM_MID, zero_codes[:], zero_scales[:])
 
         def leave_psum(copy, s, h, q0, q1):
             copy(out=z_bf[:, h, s, q0:q1], in_=z_ps[s][:].rearrange("p t (q h) -> p h q t", h=2)[:, h, q0:q1])
 
         leave_psum(vcopy, 0, 0, 0, 64)
         leave_psum(scopy, 1, 0, 0, 64)
-        leave_psum(vcopy, 0, 1, 0, 32)
+        leave_psum(vcopy, 0, 1, 0, 64)
         leave_psum(scopy, 1, 1, 0, 64)
-        leave_psum(scopy, 0, 1, 32, 64)
-        quantise(b_codes[:], b_scales[:], b_bf[:].rearrange("p l t -> p (l t)"))
 
         for h in range(2):
             quantise(z_codes[:, h], z_scales[:, h], z_bf[:, h].rearrange("p s q t -> p (s q t)"))
@@ -175,8 +177,8 @@ def tile_rows_kron_sep_kernel(tc, x, a, b, cw, out):
                     out=w_ps[c, h],
                     lhsT=z_codes[rows, h].bitcast(FP8X4),
                     lhsT_scale=z_scales[rows, h],
-                    rhs=b_codes[rows].bitcast(FP8X4),
-                    rhs_scale=b_scales[rows],
+                    rhs=codes_of(ab_mx if c == 0 else b_mx, rows).bitcast(FP8X4),
+                    rhs_scale=scales_of(ab_mx if c == 0 else b_mx, rows),
                     start=True,
                     stop=True,
                 )

@@ -8,7 +8,6 @@ FLOPS = 2 * G * (D * J * K + J * K * L)
 F32 = mybir.dt.float32
 BF16 = mybir.dt.bfloat16
 U32 = mybir.dt.uint32
-I32 = mybir.dt.int32
 U8 = mybir.dt.uint8
 FP8X4 = mybir.dt.float8_e4m3fn_x4
 
@@ -18,9 +17,6 @@ PACK = 4
 SETS = 2
 TILES = 4
 W = 128
-WARM_HEAD = 20
-WARM_LATE = 9
-WARM_MID = 8
 
 
 def tile_rows_kron_sep_kernel(tc, x, a, b, cw, out):
@@ -34,12 +30,14 @@ def tile_rows_kron_sep_kernel(tc, x, a, b, cw, out):
         raw = sb.tile([top, TILES + 1, PACK, W], F32, name="raw", align_bytes=64)
         cw_sb = sb.tile([P, 2, L], F32, name="cw_sb", align_bytes=64)
         x_bf = sb.tile([top, PACK, TILES, R, PACK], BF16, name="x_bf", align_bytes=64)
-        a_bf = sb.tile([P, K, PACK], BF16, name="a_bf", align_bytes=64)
+        a_bf = sb.tile([top, K, PACK], BF16, name="a_bf", align_bytes=64)
         z_bf = sb.tile([P, 2, SETS, K // 2, PACK], BF16, name="z_bf", align_bytes=64)
         x_codes = sb.tile([top, PACK, W], U32, name="x_codes", align_bytes=64)
         x_scales = sb.tile([top, PACK, W], U8, name="x_scales", align_bytes=64)
-        ab_mx = sb.tile([P, W + W // 4], U32, name="ab_mx", align_bytes=64)
+        ab_mx = sb.tile([top, W + W // 4], U32, name="ab_mx", align_bytes=64)
         b_mx = sb.tile([P, W + W // 4], U32, name="b_mx", align_bytes=64)
+        b_raw = sb.tile([P, PACK, L], F32, name="b_raw", align_bytes=64)
+        b_bf = sb.tile([P, L, PACK], BF16, name="b_bf", align_bytes=64)
 
         def codes_of(tile, rows):
             return tile[rows, 0:W]
@@ -47,18 +45,15 @@ def tile_rows_kron_sep_kernel(tc, x, a, b, cw, out):
         def scales_of(tile, rows):
             return tile[rows, W : W + W // 4].bitcast(U8)
 
-        every = slice(0, P)
+        used = slice(0, top)
         z_codes = sb.tile([P, 2, W], U32, name="z_codes", align_bytes=64)
         z_scales = sb.tile([P, 2, W], U8, name="z_scales", align_bytes=64)
         res = sb.tile([P, TILES, 2, L], F32, name="res", align_bytes=64)
         z_ps = [ps.tile([P, PACK, K], F32, name="z_ps%d" % s) for s in range(SETS)]
         w_first = [ps.tile([P, 2, L], F32, name="w_ps%d" % c) for c in range(TILES)]
         w_extra = ps.tile([P, L], F32, name="w_extra")
-        w_ps = {(c, 0): w_first[c][:, 0] for c in range(TILES)}
+        w_ps = {(c, h): w_first[c][:, h] for c in range(TILES) for h in range(2)}
         w_ps[0, 1] = w_extra[:]
-        w_ps[1, 1] = z_ps[0][:, 0]
-        w_ps[2, 1] = z_ps[1][:, 0]
-        w_ps[3, 1] = w_first[3][:, 1]
 
         a_rows = a.rearrange("(p u) k -> p u k", u=PACK)
         b_rows = b.rearrange("(p t) l -> p t l", t=PACK)
@@ -70,50 +65,29 @@ def tile_rows_kron_sep_kernel(tc, x, a, b, cw, out):
                 in_=x[SETS * c : SETS * (c + 1)].rearrange("s (p u) j -> (s p) u j", u=PACK),
             )
 
-        warm = sb.tile([P, 2, 8], F32, name="warm")
-        nc.gpsimd.memset(warm[:, 0], 0.0)
         load_x(0)
         for s in range(SETS):
-            nc.scalar.dma_start(out=raw[R * (s + 1) : R * (s + 2), TILES], in_=a_rows)
-        nc.sync.dma_start(out=raw[0:R, TILES], in_=b_rows)
+            nc.sync.dma_start(out=raw[R * (s + 1) : R * (s + 2), TILES], in_=a_rows)
         for c in range(1, TILES):
             load_x(c)
+        for c in range(TILES):
+            nc.sync.dma_start(out=b_raw[R * c : R * (c + 1)], in_=b_rows)
         for s in range(SETS):
             nc.sync.dma_start(out=cw_sb[64 * s : 64 * (s + 1)], in_=cw_rows)
 
-        nc.scalar.copy(out=warm[:, 1], in_=warm[:, 0])
-        zero = sb.tile([P, W * PACK // 2], F32, name="zero", align_bytes=64)
-        zero_codes = sb.tile([P, W], U32, name="zero_codes", align_bytes=64)
-        zero_scales = sb.tile([P, W], U8, name="zero_scales", align_bytes=64)
-        warm_ps = ps.tile([P, W], F32, name="warm_ps")
+        zero = sb.tile([R, W], F32, name="zero", align_bytes=64)
         nc.vector.memset(zero[:], 0.0)
-        nc.vector.memset(a_bf[top:P].rearrange("p k u -> p (k u)"), 0.0)
-        nc.vector.quantize_mx(out=zero_codes[:].bitcast(FP8X4), scales=zero_scales[:], in_=zero[:].bitcast(BF16))
 
-        def fill(c0, c1):
-            n = 2 * (c1 - c0)
-            nc.vector.tensor_copy(
-                out=raw[0:R, c0:c1].rearrange("p c (v u) j -> p (c v) (u j)", u=2),
-                in_=zero[0:R].unsqueeze(1).to_broadcast([R, n, W * PACK // 2]),
-            )
+        unused = raw[0:R].rearrange("p c u j -> p (c u) j")
 
-        fill(0, 1)
-        nc.vector.memset(ab_mx[:, W : W + W // 4], 0)
-        fill(1, 4)
+        def fill(r0, r1):
+            nc.vector.tensor_copy(out=unused[:, r0:r1], in_=zero[:].unsqueeze(1).to_broadcast([R, r1 - r0, W]))
 
-        def keep_warm(n, codes, scales):
-            for i in range(n):
-                nc.tensor.matmul_mx(
-                    out=warm_ps[:],
-                    lhsT=codes.bitcast(FP8X4),
-                    lhsT_scale=scales,
-                    rhs=codes.bitcast(FP8X4),
-                    rhs_scale=scales,
-                    start=True,
-                    stop=True,
-                )
-
-        keep_warm(WARM_HEAD, zero_codes[:], zero_scales[:])
+        last = unused[:, 14:16].rearrange("p r j -> p (r j)").bitcast(U32)
+        nc.scalar.mul(out=last, in_=last, mul=0.0)
+        fill(0, 4)
+        fill(16, 20)
+        fill(4, 14)
 
         def deal_x(copy, c, m0, m1):
             copy(
@@ -134,12 +108,9 @@ def tile_rows_kron_sep_kernel(tc, x, a, b, cw, out):
         scopy = nc.scalar.copy
 
         deal_x(scopy, 0, 0, R)
-        interleave(vcopy, a_bf[0:top], raw[:, TILES])
+        interleave(vcopy, a_bf[:], raw[:, TILES])
         deal_x(vcopy, 1, 0, R)
-        quantise(codes_of(ab_mx, every), scales_of(ab_mx, every), a_bf[:].rearrange("p k u -> p (k u)"))
-        for c in range(1, TILES):
-            nc.sync.dma_start(out=b_mx[R * c : R * (c + 1)].bitcast(I32), in_=ab_mx[0:R].bitcast(I32))
-        keep_warm(WARM_LATE, codes_of(ab_mx, every), scales_of(ab_mx, every))
+        quantise(codes_of(ab_mx, used), scales_of(ab_mx, used), a_bf[:].rearrange("p k u -> p (k u)"))
         deal_x(scopy, 2, 0, 12)
         deal_x(vcopy, 2, 12, R)
         deal_x(scopy, 3, 0, 12)
@@ -159,7 +130,8 @@ def tile_rows_kron_sep_kernel(tc, x, a, b, cw, out):
                     stop=True,
                 )
 
-        keep_warm(WARM_MID, zero_codes[:], zero_scales[:])
+        interleave(scopy, b_bf[:], b_raw[:])
+        quantise(codes_of(b_mx, slice(0, P)), scales_of(b_mx, slice(0, P)), b_bf[:].rearrange("p l u -> p (l u)"))
 
         def leave_psum(copy, s, h, q0, q1):
             copy(out=z_bf[:, h, s, q0:q1], in_=z_ps[s][:].rearrange("p t (q h) -> p h q t", h=2)[:, h, q0:q1])
@@ -171,19 +143,19 @@ def tile_rows_kron_sep_kernel(tc, x, a, b, cw, out):
 
         for h in range(2):
             quantise(z_codes[:, h], z_scales[:, h], z_bf[:, h].rearrange("p s q t -> p (s q t)"))
-            for c in ((0, 1, 2, 3), (0, 3, 1, 2))[h]:
+            for c in range(TILES):
                 rows = slice(R * c, R * (c + 1))
                 nc.tensor.matmul_mx(
                     out=w_ps[c, h],
                     lhsT=z_codes[rows, h].bitcast(FP8X4),
                     lhsT_scale=z_scales[rows, h],
-                    rhs=codes_of(ab_mx if c == 0 else b_mx, rows).bitcast(FP8X4),
-                    rhs_scale=scales_of(ab_mx if c == 0 else b_mx, rows),
+                    rhs=codes_of(b_mx, rows).bitcast(FP8X4),
+                    rhs_scale=scales_of(b_mx, rows),
                     start=True,
                     stop=True,
                 )
 
-        steps = [(0, 0, 1), (1, 0, 1), (2, 0, 1), (0, 1, 2), (3, 0, 2), (1, 1, 2), (2, 1, 2)]
+        steps = [(0, 0, 1), (0, 1, 2), (1, 0, 2), (2, 0, 2), (3, 0, 2)]
         for c, h0, h1 in steps:
             sums = w_first[c][:] if h1 - h0 == 2 else w_ps[c, h0].unsqueeze(1)
             nc.vector.tensor_tensor(out=res[:, c, h0:h1], in0=sums, in1=cw_sb[:, h0:h1], op=mybir.AluOpType.mult)

@@ -31,29 +31,25 @@ def tile_rows_kron_sep_kernel(tc, x, a, b, cw, out):
         cw_sb = sb.tile([P, 2, L], F32, name="cw_sb", align_bytes=64)
         x_bf = sb.tile([top, PACK, TILES, R, PACK], BF16, name="x_bf", align_bytes=64)
         a_bf = sb.tile([top, K, PACK], BF16, name="a_bf", align_bytes=64)
+        b_raw = sb.tile([P, PACK, L], F32, name="b_raw", align_bytes=64)
+        b_bf = sb.tile([P, L, PACK], BF16, name="b_bf", align_bytes=64)
         z_bf = sb.tile([P, 2, SETS, K // 2, PACK], BF16, name="z_bf", align_bytes=64)
         x_codes = sb.tile([top, PACK, W], U32, name="x_codes", align_bytes=64)
         x_scales = sb.tile([top, PACK, W], U8, name="x_scales", align_bytes=64)
-        ab_mx = sb.tile([top, W + W // 4], U32, name="ab_mx", align_bytes=64)
-        b_mx = sb.tile([P, W + W // 4], U32, name="b_mx", align_bytes=64)
-        b_raw = sb.tile([P, PACK, L], F32, name="b_raw", align_bytes=64)
-        b_bf = sb.tile([P, L, PACK], BF16, name="b_bf", align_bytes=64)
-
-        def codes_of(tile, rows):
-            return tile[rows, 0:W]
-
-        def scales_of(tile, rows):
-            return tile[rows, W : W + W // 4].bitcast(U8)
-
-        used = slice(0, top)
+        a_codes = sb.tile([top, W], U32, name="a_codes", align_bytes=64)
+        a_scales = sb.tile([top, W], U8, name="a_scales", align_bytes=64)
+        b_codes = sb.tile([P, W], U32, name="b_codes", align_bytes=64)
+        b_scales = sb.tile([P, W], U8, name="b_scales", align_bytes=64)
         z_codes = sb.tile([P, 2, W], U32, name="z_codes", align_bytes=64)
         z_scales = sb.tile([P, 2, W], U8, name="z_scales", align_bytes=64)
         res = sb.tile([P, TILES, 2, L], F32, name="res", align_bytes=64)
+        zero = sb.tile([P, W], F32, name="zero", align_bytes=64)
         z_ps = [ps.tile([P, PACK, K], F32, name="z_ps%d" % s) for s in range(SETS)]
-        w_first = [ps.tile([P, 2, L], F32, name="w_ps%d" % c) for c in range(TILES)]
+        w_pair = [ps.tile([P, 2, L], F32, name="w_ps%d" % c) for c in range(TILES)]
         w_extra = ps.tile([P, L], F32, name="w_extra")
-        w_ps = {(c, h): w_first[c][:, h] for c in range(TILES) for h in range(2)}
+        w_ps = {(c, h): w_pair[c][:, h] for c in range(TILES) for h in range(2)}
         w_ps[0, 1] = w_extra[:]
+        w_ps[1, 1] = z_ps[0][:, 0]
 
         a_rows = a.rearrange("(p u) k -> p u k", u=PACK)
         b_rows = b.rearrange("(p t) l -> p t l", t=PACK)
@@ -65,29 +61,31 @@ def tile_rows_kron_sep_kernel(tc, x, a, b, cw, out):
                 in_=x[SETS * c : SETS * (c + 1)].rearrange("s (p u) j -> (s p) u j", u=PACK),
             )
 
+        def load_a(queue):
+            for s in range(SETS):
+                queue.dma_start(out=raw[R * (s + 1) : R * (s + 2), TILES], in_=a_rows)
+
         load_x(0)
-        for s in range(SETS):
-            nc.sync.dma_start(out=raw[R * (s + 1) : R * (s + 2), TILES], in_=a_rows)
+        load_a(nc.sync)
         for c in range(1, TILES):
             load_x(c)
+
         for c in range(TILES):
             nc.sync.dma_start(out=b_raw[R * c : R * (c + 1)], in_=b_rows)
         for s in range(SETS):
             nc.sync.dma_start(out=cw_sb[64 * s : 64 * (s + 1)], in_=cw_rows)
 
-        zero = sb.tile([R, W], F32, name="zero", align_bytes=64)
-        nc.vector.memset(zero[:], 0.0)
-
         unused = raw[0:R].rearrange("p c u j -> p (c u) j")
 
         def fill(r0, r1):
-            nc.vector.tensor_copy(out=unused[:, r0:r1], in_=zero[:].unsqueeze(1).to_broadcast([R, r1 - r0, W]))
+            nc.vector.tensor_copy(out=unused[:, r0:r1], in_=zero[0:R].unsqueeze(1).to_broadcast([R, r1 - r0, W]))
 
+        nc.vector.memset(zero[:], 0.0)
         last = unused[:, 14:16].rearrange("p r j -> p (r j)").bitcast(U32)
         nc.scalar.mul(out=last, in_=last, mul=0.0)
-        fill(0, 4)
+        fill(0, 14)
         fill(16, 20)
-        fill(4, 14)
+
 
         def deal_x(copy, c, m0, m1):
             copy(
@@ -95,72 +93,93 @@ def tile_rows_kron_sep_kernel(tc, x, a, b, cw, out):
                 in_=raw[:, c].rearrange("p u (m t) -> p m u t", t=PACK)[:, m0:m1],
             )
 
-        def interleave(copy, dst, src):
+        def interleave(copy, dst, src, n0, n1):
             copy(
-                out=dst.rearrange("p (n i) u -> p n u i", i=PACK),
-                in_=src.rearrange("p u (n i) -> p n u i", i=PACK),
+                out=dst.rearrange("p (n i) u -> p n u i", i=PACK)[:, n0:n1],
+                in_=src.rearrange("p u (n i) -> p n u i", i=PACK)[:, n0:n1],
             )
 
         def quantise(codes, scales, values):
             nc.vector.quantize_mx(out=codes.bitcast(FP8X4), scales=scales, in_=values)
 
+        def quantise_x(t):
+            quantise(x_codes[:, t], x_scales[:, t], x_bf[:, t].rearrange("p c m u -> p (c m u)"))
+
+        def quantise_a():
+            quantise(a_codes[:], a_scales[:], a_bf[:].rearrange("p k u -> p (k u)"))
+
+        def first_product(s, t):
+            rows = slice(R * (s + 1), R * (s + 2))
+            nc.tensor.matmul_mx(
+                out=z_ps[s][:, t],
+                lhsT=x_codes[rows, t].bitcast(FP8X4),
+                lhsT_scale=x_scales[rows, t],
+                rhs=a_codes[rows].bitcast(FP8X4),
+                rhs_scale=a_scales[rows],
+                start=True,
+                stop=True,
+            )
+
         vcopy = nc.vector.tensor_copy
         scopy = nc.scalar.copy
 
         deal_x(scopy, 0, 0, R)
-        interleave(vcopy, a_bf[:], raw[:, TILES])
+        interleave(vcopy, a_bf[:], raw[:, TILES], 0, R)
         deal_x(vcopy, 1, 0, R)
-        quantise(codes_of(ab_mx, used), scales_of(ab_mx, used), a_bf[:].rearrange("p k u -> p (k u)"))
-        deal_x(scopy, 2, 0, 12)
-        deal_x(vcopy, 2, 12, R)
-        deal_x(scopy, 3, 0, 12)
-        deal_x(vcopy, 3, 12, R)
-
+        for c in range(2, TILES):
+            deal_x(scopy, c, 0, 12)
+            deal_x(vcopy, c, 12, R)
+        quantise_a()
         for t in range(PACK):
-            quantise(x_codes[:, t], x_scales[:, t], x_bf[:, t].rearrange("p c m u -> p (c m u)"))
-            for s in range(SETS):
-                rows = slice(R * (s + 1), R * (s + 2))
-                nc.tensor.matmul_mx(
-                    out=z_ps[s][:, t],
-                    lhsT=x_codes[rows, t].bitcast(FP8X4),
-                    lhsT_scale=x_scales[rows, t],
-                    rhs=codes_of(ab_mx, rows).bitcast(FP8X4),
-                    rhs_scale=scales_of(ab_mx, rows),
-                    start=True,
-                    stop=True,
-                )
+            quantise_x(t)
+        for s, t in ((0, 0), (1, 0), (0, 1), (0, 2), (1, 1), (0, 3), (1, 2), (1, 3)):
+            first_product(s, t)
 
-        interleave(scopy, b_bf[:], b_raw[:])
-        quantise(codes_of(b_mx, slice(0, P)), scales_of(b_mx, slice(0, P)), b_bf[:].rearrange("p l u -> p (l u)"))
+        interleave(scopy, b_bf[:], b_raw[:], 0, 12)
+        interleave(vcopy, b_bf[:], b_raw[:], 12, R)
+        quantise(b_codes[:], b_scales[:], b_bf[:].rearrange("p l u -> p (l u)"))
 
         def leave_psum(copy, s, h, q0, q1):
             copy(out=z_bf[:, h, s, q0:q1], in_=z_ps[s][:].rearrange("p t (q h) -> p h q t", h=2)[:, h, q0:q1])
 
-        leave_psum(vcopy, 0, 0, 0, 64)
-        leave_psum(scopy, 1, 0, 0, 64)
-        leave_psum(vcopy, 0, 1, 0, 64)
-        leave_psum(scopy, 1, 1, 0, 64)
+        def quantise_z(h):
+            quantise(z_codes[:, h], z_scales[:, h], z_bf[:, h].rearrange("p s q t -> p (s q t)"))
+
+        def second_product(c, h):
+            rows = slice(R * c, R * (c + 1))
+            nc.tensor.matmul_mx(
+                out=w_ps[c, h],
+                lhsT=z_codes[rows, h].bitcast(FP8X4),
+                lhsT_scale=z_scales[rows, h],
+                rhs=b_codes[rows].bitcast(FP8X4),
+                rhs_scale=b_scales[rows],
+                start=True,
+                stop=True,
+            )
 
         for h in range(2):
-            quantise(z_codes[:, h], z_scales[:, h], z_bf[:, h].rearrange("p s q t -> p (s q t)"))
-            for c in range(TILES):
-                rows = slice(R * c, R * (c + 1))
-                nc.tensor.matmul_mx(
-                    out=w_ps[c, h],
-                    lhsT=z_codes[rows, h].bitcast(FP8X4),
-                    lhsT_scale=z_scales[rows, h],
-                    rhs=codes_of(b_mx, rows).bitcast(FP8X4),
-                    rhs_scale=scales_of(b_mx, rows),
-                    start=True,
-                    stop=True,
-                )
+            leave_psum(vcopy, 0, h, 0, 64)
+            leave_psum(scopy, 1, h, 0, 64)
+        for h in range(2):
+            quantise_z(h)
+        for c, h in ((0, 0), (1, 0), (0, 1), (1, 1), (2, 0), (2, 1), (3, 0), (3, 1)):
+            second_product(c, h)
 
-        steps = [(0, 0, 1), (0, 1, 2), (1, 0, 2), (2, 0, 2), (3, 0, 2)]
-        for c, h0, h1 in steps:
-            sums = w_first[c][:] if h1 - h0 == 2 else w_ps[c, h0].unsqueeze(1)
+        def weigh(c, h0, h1):
+            sums = w_pair[c][:] if h1 - h0 == 2 else w_ps[c, h0].unsqueeze(1)
             nc.vector.tensor_tensor(out=res[:, c, h0:h1], in0=sums, in1=cw_sb[:, h0:h1], op=mybir.AluOpType.mult)
-            if h1 == 2:
-                nc.sync.dma_start(
-                    out=out[SETS * c : SETS * (c + 1)].rearrange("s (q h) l -> (s q) h l", h=2),
-                    in_=res[:, c],
-                )
+
+        def store(queue, c, h0, h1):
+            queue.dma_start(
+                out=out[SETS * c : SETS * (c + 1)].rearrange("s (q h) l -> (s q) h l", h=2)[:, h0:h1],
+                in_=res[:, c, h0:h1],
+            )
+
+        weigh(0, 0, 1)
+        weigh(1, 0, 1)
+        for c in range(2):
+            weigh(c, 1, 2)
+            store(nc.sync, c, 0, 2)
+        for c in range(2, TILES):
+            weigh(c, 0, 2)
+            store(nc.sync, c, 0, 2)

@@ -55,20 +55,20 @@ def tile_rows_kron_sep_kernel(tc, x, a, b, cw, out):
         b_rows = b.rearrange("(p t) l -> p t l", t=PACK)
         cw_rows = cw.rearrange("(q h) l -> q h l", h=2)
 
-        def load_x(c):
+        def load_x(c0, c1):
             nc.sync.dma_start(
-                out=raw[R:top, c],
-                in_=x[SETS * c : SETS * (c + 1)].rearrange("s (p u) j -> (s p) u j", u=PACK),
+                out=raw[R:top, c0:c1].rearrange("p c u j -> p c (u j)"),
+                in_=x.rearrange("(c s) (p u) j -> (s p) c (u j)", s=SETS, u=PACK)[:, c0:c1],
             )
 
         def load_a(queue):
             for s in range(SETS):
                 queue.dma_start(out=raw[R * (s + 1) : R * (s + 2), TILES], in_=a_rows)
 
-        load_x(0)
+        load_x(0, 2)
         load_a(nc.sync)
-        for c in range(1, TILES):
-            load_x(c)
+        for c in range(2, TILES):
+            load_x(c, c + 1)
 
         for c in range(TILES):
             nc.sync.dma_start(out=b_raw[R * c : R * (c + 1)], in_=b_rows)
@@ -124,8 +124,8 @@ def tile_rows_kron_sep_kernel(tc, x, a, b, cw, out):
         scopy = nc.scalar.copy
 
         deal_x(scopy, 0, 0, R)
-        interleave(vcopy, a_bf[:], raw[:, TILES], 0, R)
         deal_x(vcopy, 1, 0, R)
+        interleave(vcopy, a_bf[:], raw[:, TILES], 0, R)
         for c in range(2, TILES):
             deal_x(scopy, c, 0, 12)
             deal_x(vcopy, c, 12, R)
@@ -176,10 +176,12 @@ def tile_rows_kron_sep_kernel(tc, x, a, b, cw, out):
             )
 
         weigh(0, 0, 1)
+        store(nc.sync, 0, 0, 1)
         weigh(1, 0, 1)
-        for c in range(2):
-            weigh(c, 1, 2)
-            store(nc.sync, c, 0, 2)
+        weigh(0, 1, 2)
+        store(nc.sync, 0, 1, 2)
+        weigh(1, 1, 2)
+        store(nc.sync, 1, 0, 2)
         for c in range(2, TILES):
             weigh(c, 0, 2)
             store(nc.sync, c, 0, 2)

@@ -16,7 +16,12 @@ R = 32
 PACK = 4
 SETS = 2
 TILES = 4
+HALVES = 2
 W = 128
+TOP = R + SETS * R
+A_SLOT = TILES
+SCALAR_SHARE = 12
+SCALAR_ZEROS = 64
 
 
 def tile_rows_kron_sep_kernel(tc, x, a, b, cw, out):
@@ -26,51 +31,49 @@ def tile_rows_kron_sep_kernel(tc, x, a, b, cw, out):
         ps = ctx.enter_context(tc.psum_pool(name="ps", bufs=1))
         ctx.enter_context(tc.manual_schedule())
 
-        top = R + SETS * R
-        raw = sb.tile([top, TILES + 1, PACK, W], F32, name="raw", align_bytes=64)
-        cw_sb = sb.tile([P, 2, L], F32, name="cw_sb", align_bytes=64)
-        x_bf = sb.tile([top, PACK, TILES, R, PACK], BF16, name="x_bf", align_bytes=64)
-        a_bf = sb.tile([top, K, PACK], BF16, name="a_bf", align_bytes=64)
+        raw = sb.tile([TOP, TILES + 1, PACK, W], F32, name="raw", align_bytes=64)
+        cw_sb = sb.tile([P, HALVES, L], F32, name="cw_sb", align_bytes=64)
+        x_bf = sb.tile([TOP, PACK, TILES, R, PACK], BF16, name="x_bf", align_bytes=64)
+        a_bf = sb.tile([TOP, K, PACK], BF16, name="a_bf", align_bytes=64)
         b_raw = sb.tile([P, PACK, L], F32, name="b_raw", align_bytes=64)
         b_bf = sb.tile([P, L, PACK], BF16, name="b_bf", align_bytes=64)
-        z_bf = sb.tile([P, 2, SETS, K // 2, PACK], BF16, name="z_bf", align_bytes=64)
-        x_codes = sb.tile([top, PACK, W], U32, name="x_codes", align_bytes=64)
-        x_scales = sb.tile([top, PACK, W], U8, name="x_scales", align_bytes=64)
-        a_codes = sb.tile([top, W], U32, name="a_codes", align_bytes=64)
-        a_scales = sb.tile([top, W], U8, name="a_scales", align_bytes=64)
+        z_bf = sb.tile([P, HALVES, SETS, K // HALVES, PACK], BF16, name="z_bf", align_bytes=64)
+        x_codes = sb.tile([TOP, PACK, W], U32, name="x_codes", align_bytes=64)
+        x_scales = sb.tile([TOP, PACK, W], U8, name="x_scales", align_bytes=64)
+        a_codes = sb.tile([TOP, W], U32, name="a_codes", align_bytes=64)
+        a_scales = sb.tile([TOP, W], U8, name="a_scales", align_bytes=64)
         b_codes = sb.tile([P, W], U32, name="b_codes", align_bytes=64)
         b_scales = sb.tile([P, W], U8, name="b_scales", align_bytes=64)
-        z_codes = sb.tile([P, 2, W], U32, name="z_codes", align_bytes=64)
-        z_scales = sb.tile([P, 2, W], U8, name="z_scales", align_bytes=64)
-        res = sb.tile([P, TILES, 2, L], F32, name="res", align_bytes=64)
+        z_codes = sb.tile([P, HALVES, W], U32, name="z_codes", align_bytes=64)
+        z_scales = sb.tile([P, HALVES, W], U8, name="z_scales", align_bytes=64)
+        res = sb.tile([P, TILES, HALVES, L], F32, name="res", align_bytes=64)
         zero = sb.tile([P, W], F32, name="zero", align_bytes=64)
+
         z_ps = [ps.tile([P, PACK, K], F32, name="z_ps%d" % s) for s in range(SETS)]
-        w_pair = [ps.tile([P, 2, L], F32, name="w_ps%d" % c) for c in range(TILES)]
-        w_extra = ps.tile([P, L], F32, name="w_extra")
-        w_ps = {(c, h): w_pair[c][:, h] for c in range(TILES) for h in range(2)}
-        w_ps[0, 1] = w_extra[:]
+        w_pair = [ps.tile([P, HALVES, L], F32, name="w_ps%d" % c) for c in range(TILES)]
+        w_odd_first = ps.tile([P, L], F32, name="w_odd_first")
+        w_ps = {(c, h): w_pair[c][:, h] for c in range(TILES) for h in range(HALVES)}
+        w_ps[0, 1] = w_odd_first[:]
         w_ps[1, 1] = z_ps[0][:, 0]
+        w_odd_last = ps.tile([P, L], F32, name="w_odd_last")
+        w_ps[3, 1] = w_odd_last[:]
 
         a_rows = a.rearrange("(p u) k -> p u k", u=PACK)
         b_rows = b.rearrange("(p t) l -> p t l", t=PACK)
-        cw_rows = cw.rearrange("(q h) l -> q h l", h=2)
+        cw_rows = cw.rearrange("(q h) l -> q h l", h=HALVES)
 
         def load_x(c0, c1):
             nc.sync.dma_start(
-                out=raw[R:top, c0:c1].rearrange("p c u j -> p c (u j)"),
+                out=raw[R:TOP, c0:c1].rearrange("p c u j -> p c (u j)"),
                 in_=x.rearrange("(c s) (p u) j -> (s p) c (u j)", s=SETS, u=PACK)[:, c0:c1],
             )
 
-        def load_a(queue):
-            for s in range(SETS):
-                queue.dma_start(out=raw[R * (s + 1) : R * (s + 2), TILES], in_=a_rows)
-
         load_x(0, 2)
-        load_a(nc.sync)
+        for s in range(SETS):
+            nc.sync.dma_start(out=raw[R * (s + 1) : R * (s + 2), A_SLOT], in_=a_rows)
         for c in range(2, TILES):
             load_x(c, c + 1)
-
-        for c in range(TILES):
+        for c in (0, 2, 1, 3):
             nc.sync.dma_start(out=b_raw[R * c : R * (c + 1)], in_=b_rows)
         for s in range(SETS):
             nc.sync.dma_start(out=cw_sb[64 * s : 64 * (s + 1)], in_=cw_rows)
@@ -81,11 +84,16 @@ def tile_rows_kron_sep_kernel(tc, x, a, b, cw, out):
             nc.vector.tensor_copy(out=unused[:, r0:r1], in_=zero[0:R].unsqueeze(1).to_broadcast([R, r1 - r0, W]))
 
         nc.vector.memset(zero[:], 0.0)
-        last = unused[:, 14:16].rearrange("p r j -> p (r j)").bitcast(U32)
-        nc.scalar.mul(out=last, in_=last, mul=0.0)
+        shared_rows = unused[:, 14:16].rearrange("p r j -> p (r j)")
+        cut = 2 * W - SCALAR_ZEROS
+        scalar_words = shared_rows[:, cut:].bitcast(U32)
+        nc.scalar.mul(out=scalar_words, in_=scalar_words, mul=0.0)
         fill(0, 14)
         fill(16, 20)
-
+        nc.vector.tensor_copy(
+            out=shared_rows[:, 0:cut].rearrange("p (r j) -> p r j", r=2),
+            in_=zero[0:R, 0 : cut // 2].unsqueeze(1).to_broadcast([R, 2, cut // 2]),
+        )
 
         def deal_x(copy, c, m0, m1):
             copy(
@@ -102,20 +110,14 @@ def tile_rows_kron_sep_kernel(tc, x, a, b, cw, out):
         def quantise(codes, scales, values):
             nc.vector.quantize_mx(out=codes.bitcast(FP8X4), scales=scales, in_=values)
 
-        def quantise_x(t):
-            quantise(x_codes[:, t], x_scales[:, t], x_bf[:, t].rearrange("p c m u -> p (c m u)"))
-
-        def quantise_a():
-            quantise(a_codes[:], a_scales[:], a_bf[:].rearrange("p k u -> p (k u)"))
-
-        def first_product(s, t):
-            rows = slice(R * (s + 1), R * (s + 2))
+        def product(sums, tile, codes, scales, moving_codes, moving_scales):
+            rows = slice(R * tile, R * (tile + 1))
             nc.tensor.matmul_mx(
-                out=z_ps[s][:, t],
-                lhsT=x_codes[rows, t].bitcast(FP8X4),
-                lhsT_scale=x_scales[rows, t],
-                rhs=a_codes[rows].bitcast(FP8X4),
-                rhs_scale=a_scales[rows],
+                out=sums,
+                lhsT=codes[rows].bitcast(FP8X4),
+                lhsT_scale=scales[rows],
+                rhs=moving_codes[rows].bitcast(FP8X4),
+                rhs_scale=moving_scales[rows],
                 start=True,
                 stop=True,
             )
@@ -125,63 +127,56 @@ def tile_rows_kron_sep_kernel(tc, x, a, b, cw, out):
 
         deal_x(scopy, 0, 0, R)
         deal_x(vcopy, 1, 0, R)
-        interleave(vcopy, a_bf[:], raw[:, TILES], 0, R)
+        interleave(vcopy, a_bf[:], raw[:, A_SLOT], 0, R)
         for c in range(2, TILES):
-            deal_x(scopy, c, 0, 12)
-            deal_x(vcopy, c, 12, R)
-        quantise_a()
+            deal_x(scopy, c, 0, SCALAR_SHARE)
+            deal_x(vcopy, c, SCALAR_SHARE, R)
+        quantise(a_codes[:], a_scales[:], a_bf[:].rearrange("p k u -> p (k u)"))
         for t in range(PACK):
-            quantise_x(t)
+            quantise(x_codes[:, t], x_scales[:, t], x_bf[:, t].rearrange("p c m u -> p (c m u)"))
+
         for s, t in ((0, 0), (1, 0), (0, 1), (0, 2), (1, 1), (0, 3), (1, 2), (1, 3)):
-            first_product(s, t)
+            product(z_ps[s][:, t], s + 1, x_codes[:, t], x_scales[:, t], a_codes, a_scales)
 
-        interleave(scopy, b_bf[:], b_raw[:], 0, 12)
-        interleave(vcopy, b_bf[:], b_raw[:], 12, R)
-        quantise(b_codes[:], b_scales[:], b_bf[:].rearrange("p l u -> p (l u)"))
+        interleave(scopy, b_bf[:], b_raw[:], 0, SCALAR_SHARE)
+        interleave(vcopy, b_bf[:], b_raw[:], SCALAR_SHARE, R)
+        quantise(b_codes[:], b_scales[:], b_bf[:].rearrange("p l t -> p (l t)"))
 
-        def leave_psum(copy, s, h, q0, q1):
-            copy(out=z_bf[:, h, s, q0:q1], in_=z_ps[s][:].rearrange("p t (q h) -> p h q t", h=2)[:, h, q0:q1])
-
-        def quantise_z(h):
+        for h in range(HALVES):
+            for s, copy in enumerate((vcopy, scopy)):
+                copy(out=z_bf[:, h, s], in_=z_ps[s][:].rearrange("p t (q h) -> p h q t", h=HALVES)[:, h])
+        for h in range(HALVES):
             quantise(z_codes[:, h], z_scales[:, h], z_bf[:, h].rearrange("p s q t -> p (s q t)"))
 
-        def second_product(c, h):
-            rows = slice(R * c, R * (c + 1))
-            nc.tensor.matmul_mx(
-                out=w_ps[c, h],
-                lhsT=z_codes[rows, h].bitcast(FP8X4),
-                lhsT_scale=z_scales[rows, h],
-                rhs=b_codes[rows].bitcast(FP8X4),
-                rhs_scale=b_scales[rows],
-                start=True,
-                stop=True,
+        for c, h in ((0, 0), (1, 0), (0, 1), (1, 1), (2, 0), (2, 1), (3, 0), (3, 1)):
+            product(w_ps[c, h], c, z_codes[:, h], z_scales[:, h], b_codes, b_scales)
+
+        def weigh(c, h):
+            nc.vector.tensor_tensor(
+                out=res[:, c, h : h + 1],
+                in0=w_ps[c, h].unsqueeze(1),
+                in1=cw_sb[:, h : h + 1],
+                op=mybir.AluOpType.mult,
             )
 
-        for h in range(2):
-            leave_psum(vcopy, 0, h, 0, 64)
-            leave_psum(scopy, 1, h, 0, 64)
-        for h in range(2):
-            quantise_z(h)
-        for c, h in ((0, 0), (1, 0), (0, 1), (1, 1), (2, 0), (2, 1), (3, 0), (3, 1)):
-            second_product(c, h)
+        def weigh_both(c):
+            nc.vector.tensor_tensor(out=res[:, c], in0=w_pair[c][:], in1=cw_sb[:], op=mybir.AluOpType.mult)
 
-        def weigh(c, h0, h1):
-            sums = w_pair[c][:] if h1 - h0 == 2 else w_ps[c, h0].unsqueeze(1)
-            nc.vector.tensor_tensor(out=res[:, c, h0:h1], in0=sums, in1=cw_sb[:, h0:h1], op=mybir.AluOpType.mult)
-
-        def store(queue, c, h0, h1):
-            queue.dma_start(
-                out=out[SETS * c : SETS * (c + 1)].rearrange("s (q h) l -> (s q) h l", h=2)[:, h0:h1],
+        def store(c, h0, h1):
+            nc.sync.dma_start(
+                out=out[SETS * c : SETS * (c + 1)].rearrange("s (q h) l -> (s q) h l", h=HALVES)[:, h0:h1],
                 in_=res[:, c, h0:h1],
             )
 
-        weigh(0, 0, 1)
-        store(nc.sync, 0, 0, 1)
-        weigh(1, 0, 1)
-        weigh(0, 1, 2)
-        store(nc.sync, 0, 1, 2)
-        weigh(1, 1, 2)
-        store(nc.sync, 1, 0, 2)
-        for c in range(2, TILES):
-            weigh(c, 0, 2)
-            store(nc.sync, c, 0, 2)
+        weigh(0, 0)
+        store(0, 0, 1)
+        weigh(1, 0)
+        weigh(0, 1)
+        store(0, 1, 2)
+        weigh(1, 1)
+        store(1, 0, 2)
+        weigh_both(2)
+        store(2, 0, 2)
+        for h in range(HALVES):
+            weigh(3, h)
+        store(3, 0, 2)

@@ -20,7 +20,7 @@ HALVES = 2
 W = 128
 TOP = R + SETS * R
 A_SLOT = TILES
-SCALAR_SHARE = 12
+SCALAR_SHARE = 14
 SCALAR_ZEROS = 64
 
 
@@ -55,8 +55,7 @@ def tile_rows_kron_sep_kernel(tc, x, a, b, cw, out):
         w_ps = {(c, h): w_pair[c][:, h] for c in range(TILES) for h in range(HALVES)}
         w_ps[0, 1] = w_odd_first[:]
         w_ps[1, 1] = z_ps[0][:, 0]
-        w_odd_last = ps.tile([P, L], F32, name="w_odd_last")
-        w_ps[3, 1] = w_odd_last[:]
+        w_ps[2, 1] = z_ps[1][:, 0]
 
         a_rows = a.rearrange("(p u) k -> p u k", u=PACK)
         b_rows = b.rearrange("(p t) l -> p t l", t=PACK)
@@ -95,10 +94,10 @@ def tile_rows_kron_sep_kernel(tc, x, a, b, cw, out):
             in_=zero[0:R, 0 : cut // 2].unsqueeze(1).to_broadcast([R, 2, cut // 2]),
         )
 
-        def deal_x(copy, c, m0, m1):
+        def deal_x(copy, c0, c1, t0):
             copy(
-                out=x_bf[:, :, c, m0:m1].rearrange("p t m u -> p m u t"),
-                in_=raw[:, c].rearrange("p u (m t) -> p m u t", t=PACK)[:, m0:m1],
+                out=x_bf[:, t0 : t0 + 2, c0:c1].rearrange("p t c m u -> p c m u t"),
+                in_=raw[:, c0:c1].rearrange("p c u (m t) -> p c m u t", t=PACK)[:, :, :, :, t0 : t0 + 2],
             )
 
         def interleave(copy, dst, src, n0, n1):
@@ -125,18 +124,21 @@ def tile_rows_kron_sep_kernel(tc, x, a, b, cw, out):
         vcopy = nc.vector.tensor_copy
         scopy = nc.scalar.copy
 
-        deal_x(scopy, 0, 0, R)
-        deal_x(vcopy, 1, 0, R)
-        interleave(vcopy, a_bf[:], raw[:, A_SLOT], 0, R)
+        deal_x(vcopy, 0, 2, 0)
+        deal_x(scopy, 0, 1, 2)
+        interleave(scopy, a_bf[:], raw[:, A_SLOT], 0, SCALAR_SHARE)
+        interleave(vcopy, a_bf[:], raw[:, A_SLOT], SCALAR_SHARE, R)
+        deal_x(scopy, 1, 2, 2)
         for c in range(2, TILES):
-            deal_x(scopy, c, 0, SCALAR_SHARE)
-            deal_x(vcopy, c, SCALAR_SHARE, R)
+            deal_x(vcopy, c, c + 1, 0)
+            deal_x(scopy, c, c + 1, 2)
         quantise(a_codes[:], a_scales[:], a_bf[:].rearrange("p k u -> p (k u)"))
         for t in range(PACK):
             quantise(x_codes[:, t], x_scales[:, t], x_bf[:, t].rearrange("p c m u -> p (c m u)"))
 
-        for s, t in ((0, 0), (1, 0), (0, 1), (0, 2), (1, 1), (0, 3), (1, 2), (1, 3)):
-            product(z_ps[s][:, t], s + 1, x_codes[:, t], x_scales[:, t], a_codes, a_scales)
+        for t in range(PACK):
+            for s in range(SETS):
+                product(z_ps[s][:, t], s + 1, x_codes[:, t], x_scales[:, t], a_codes, a_scales)
 
         interleave(scopy, b_bf[:], b_raw[:], 0, SCALAR_SHARE)
         interleave(vcopy, b_bf[:], b_raw[:], SCALAR_SHARE, R)
@@ -148,8 +150,9 @@ def tile_rows_kron_sep_kernel(tc, x, a, b, cw, out):
         for h in range(HALVES):
             quantise(z_codes[:, h], z_scales[:, h], z_bf[:, h].rearrange("p s q t -> p (s q t)"))
 
-        for c, h in ((0, 0), (1, 0), (0, 1), (1, 1), (2, 0), (2, 1), (3, 0), (3, 1)):
-            product(w_ps[c, h], c, z_codes[:, h], z_scales[:, h], b_codes, b_scales)
+        for h in range(HALVES):
+            for c in range(TILES):
+                product(w_ps[c, h], c, z_codes[:, h], z_scales[:, h], b_codes, b_scales)
 
         def weigh(c, h):
             nc.vector.tensor_tensor(
@@ -171,12 +174,11 @@ def tile_rows_kron_sep_kernel(tc, x, a, b, cw, out):
         weigh(0, 0)
         store(0, 0, 1)
         weigh(1, 0)
+        weigh(2, 0)
         weigh(0, 1)
         store(0, 1, 2)
-        weigh(1, 1)
-        store(1, 0, 2)
-        weigh_both(2)
-        store(2, 0, 2)
-        for h in range(HALVES):
-            weigh(3, h)
+        for c in (1, 2):
+            weigh(c, 1)
+            store(c, 0, 2)
+        weigh_both(3)
         store(3, 0, 2)

@@ -33,13 +33,13 @@ def tile_rows_kron_sep_kernel(tc, x, a, b, cw, out):
 
         raw = sb.tile([TOP, TILES + 1, PACK, W], F32, name="raw", align_bytes=64)
         cw_sb = sb.tile([P, HALVES, L], F32, name="cw_sb", align_bytes=64)
-        x_bf = sb.tile([TOP, PACK, TILES, R, PACK], BF16, name="x_bf", align_bytes=64)
+        x_bf = sb.tile([P, PACK, TILES, R, PACK], BF16, name="x_bf", align_bytes=64)
         a_bf = sb.tile([TOP, K, PACK], BF16, name="a_bf", align_bytes=64)
         b_raw = sb.tile([P, PACK, L], F32, name="b_raw", align_bytes=64)
         b_bf = sb.tile([P, L, PACK], BF16, name="b_bf", align_bytes=64)
         z_bf = sb.tile([P, HALVES, SETS, K // HALVES, PACK], BF16, name="z_bf", align_bytes=64)
-        x_codes = sb.tile([TOP, PACK, W], U32, name="x_codes", align_bytes=64)
-        x_scales = sb.tile([TOP, PACK, W], U8, name="x_scales", align_bytes=64)
+        x_codes = sb.tile([P, PACK, W], U32, name="x_codes", align_bytes=64)
+        x_scales = sb.tile([P, PACK, W], U8, name="x_scales", align_bytes=64)
         a_codes = sb.tile([TOP, W], U32, name="a_codes", align_bytes=64)
         a_scales = sb.tile([TOP, W], U8, name="a_scales", align_bytes=64)
         b_codes = sb.tile([P, W], U32, name="b_codes", align_bytes=64)
@@ -55,7 +55,6 @@ def tile_rows_kron_sep_kernel(tc, x, a, b, cw, out):
         w_ps = {(c, h): w_pair[c][:, h] for c in range(TILES) for h in range(HALVES)}
         w_ps[0, 1] = w_odd_first[:]
         w_ps[1, 1] = z_ps[0][:, 0]
-        w_ps[2, 1] = z_ps[1][:, 0]
 
         a_rows = a.rearrange("(p u) k -> p u k", u=PACK)
         b_rows = b.rearrange("(p t) l -> p t l", t=PACK)
@@ -87,6 +86,7 @@ def tile_rows_kron_sep_kernel(tc, x, a, b, cw, out):
         cut = 2 * W - SCALAR_ZEROS
         scalar_words = shared_rows[:, cut:].bitcast(U32)
         nc.scalar.mul(out=scalar_words, in_=scalar_words, mul=0.0)
+        nc.vector.memset(x_bf[TOP:P, 0:2].rearrange("p t c m u -> p (t c m u)").bitcast(U32), 0)
         fill(0, 14)
         fill(16, 20)
         nc.vector.tensor_copy(
@@ -96,7 +96,7 @@ def tile_rows_kron_sep_kernel(tc, x, a, b, cw, out):
 
         def deal_x(copy, c0, c1, t0):
             copy(
-                out=x_bf[:, t0 : t0 + 2, c0:c1].rearrange("p t c m u -> p c m u t"),
+                out=x_bf[0:TOP, t0 : t0 + 2, c0:c1].rearrange("p t c m u -> p c m u t"),
                 in_=raw[:, c0:c1].rearrange("p c u (m t) -> p c m u t", t=PACK)[:, :, :, :, t0 : t0 + 2],
             )
 
@@ -124,17 +124,26 @@ def tile_rows_kron_sep_kernel(tc, x, a, b, cw, out):
         vcopy = nc.vector.tensor_copy
         scopy = nc.scalar.copy
 
+        def quantise_half(t, c0):
+            cols = slice(R * c0, R * (c0 + 2))
+            quantise(x_codes[:, t, cols], x_scales[:, t, cols], x_bf[:, t, c0 : c0 + 2].rearrange("p c m u -> p (c m u)"))
+
         deal_x(vcopy, 0, 2, 0)
         deal_x(scopy, 0, 1, 2)
         interleave(scopy, a_bf[:], raw[:, A_SLOT], 0, SCALAR_SHARE)
         interleave(vcopy, a_bf[:], raw[:, A_SLOT], SCALAR_SHARE, R)
         deal_x(scopy, 1, 2, 2)
-        for c in range(2, TILES):
-            deal_x(vcopy, c, c + 1, 0)
-            deal_x(scopy, c, c + 1, 2)
+        deal_x(vcopy, 2, 3, 0)
+        deal_x(scopy, 2, 3, 2)
+        for t in range(2):
+            quantise_half(t, 0)
+        deal_x(vcopy, 3, 4, 0)
+        deal_x(scopy, 3, 4, 2)
         quantise(a_codes[:], a_scales[:], a_bf[:].rearrange("p k u -> p (k u)"))
-        for t in range(PACK):
-            quantise(x_codes[:, t], x_scales[:, t], x_bf[:, t].rearrange("p c m u -> p (c m u)"))
+        for t in range(2):
+            quantise_half(t, 2)
+        for t in range(2, PACK):
+            quantise(x_codes[0:TOP, t], x_scales[0:TOP, t], x_bf[0:TOP, t].rearrange("p c m u -> p (c m u)"))
 
         for t in range(PACK):
             for s in range(SETS):
@@ -150,8 +159,8 @@ def tile_rows_kron_sep_kernel(tc, x, a, b, cw, out):
         for h in range(HALVES):
             quantise(z_codes[:, h], z_scales[:, h], z_bf[:, h].rearrange("p s q t -> p (s q t)"))
 
-        for h in range(HALVES):
-            for c in range(TILES):
+        for c0, h in ((0, 0), (0, 1), (2, 0), (2, 1)):
+            for c in (c0, c0 + 1):
                 product(w_ps[c, h], c, z_codes[:, h], z_scales[:, h], b_codes, b_scales)
 
         def weigh(c, h):
@@ -174,11 +183,10 @@ def tile_rows_kron_sep_kernel(tc, x, a, b, cw, out):
         weigh(0, 0)
         store(0, 0, 1)
         weigh(1, 0)
-        weigh(2, 0)
         weigh(0, 1)
         store(0, 1, 2)
-        for c in (1, 2):
-            weigh(c, 1)
+        weigh(1, 1)
+        store(1, 0, 2)
+        for c in range(2, TILES):
+            weigh_both(c)
             store(c, 0, 2)
-        weigh_both(3)
-        store(3, 0, 2)

@@ -17,9 +17,11 @@ PACK = 4
 SETS = 2
 TILES = 4
 HALVES = 2
+PAIRS = K // HALVES
 W = 128
 TOP = R + SETS * R
 A_SLOT = TILES
+EARLY = 2
 SCALAR_SHARE = 14
 SCALAR_ZEROS = 64
 
@@ -37,7 +39,7 @@ def tile_rows_kron_sep_kernel(tc, x, a, b, cw, out):
         a_bf = sb.tile([TOP, K, PACK], BF16, name="a_bf", align_bytes=64)
         b_raw = sb.tile([P, PACK, L], F32, name="b_raw", align_bytes=64)
         b_bf = sb.tile([P, L, PACK], BF16, name="b_bf", align_bytes=64)
-        z_bf = sb.tile([P, HALVES, SETS, K // HALVES, PACK], BF16, name="z_bf", align_bytes=64)
+        z_bf = sb.tile([P, HALVES, SETS, PAIRS, PACK], BF16, name="z_bf", align_bytes=64)
         x_codes = sb.tile([P, PACK, W], U32, name="x_codes", align_bytes=64)
         x_scales = sb.tile([P, PACK, W], U8, name="x_scales", align_bytes=64)
         a_codes = sb.tile([TOP, W], U32, name="a_codes", align_bytes=64)
@@ -47,14 +49,14 @@ def tile_rows_kron_sep_kernel(tc, x, a, b, cw, out):
         z_codes = sb.tile([P, HALVES, W], U32, name="z_codes", align_bytes=64)
         z_scales = sb.tile([P, HALVES, W], U8, name="z_scales", align_bytes=64)
         res = sb.tile([P, TILES, HALVES, L], F32, name="res", align_bytes=64)
-        zero = sb.tile([P, W], F32, name="zero", align_bytes=64)
+        zero = sb.tile([R, W], F32, name="zero", align_bytes=64)
 
         z_ps = [ps.tile([P, PACK, K], F32, name="z_ps%d" % s) for s in range(SETS)]
-        w_pair = [ps.tile([P, HALVES, L], F32, name="w_ps%d" % c) for c in range(TILES)]
+        w_even = [ps.tile([P, L], F32, name="w_even%d" % c) for c in range(TILES)]
         w_odd_first = ps.tile([P, L], F32, name="w_odd_first")
-        w_ps = {(c, h): w_pair[c][:, h] for c in range(TILES) for h in range(HALVES)}
-        w_ps[0, 1] = w_odd_first[:]
-        w_ps[1, 1] = z_ps[0][:, 0]
+        w_odd_last = ps.tile([P, L], F32, name="w_odd_last")
+        w_odd = [w_odd_first[:], z_ps[0][:, 0], z_ps[1][:, 0], w_odd_last[:]]
+        w_ps = [[w_even[c][:], w_odd[c]] for c in range(TILES)]
 
         a_rows = a.rearrange("(p u) k -> p u k", u=PACK)
         b_rows = b.rearrange("(p t) l -> p t l", t=PACK)
@@ -74,24 +76,25 @@ def tile_rows_kron_sep_kernel(tc, x, a, b, cw, out):
         for c in (0, 2, 1, 3):
             nc.sync.dma_start(out=b_raw[R * c : R * (c + 1)], in_=b_rows)
         for s in range(SETS):
-            nc.sync.dma_start(out=cw_sb[64 * s : 64 * (s + 1)], in_=cw_rows)
+            nc.sync.dma_start(out=cw_sb[PAIRS * s : PAIRS * (s + 1)], in_=cw_rows)
 
         unused = raw[0:R].rearrange("p c u j -> p (c u) j")
+        shared_from = PACK * TILES - 2
 
         def fill(r0, r1):
-            nc.vector.tensor_copy(out=unused[:, r0:r1], in_=zero[0:R].unsqueeze(1).to_broadcast([R, r1 - r0, W]))
+            nc.vector.tensor_copy(out=unused[:, r0:r1], in_=zero[:].unsqueeze(1).to_broadcast([R, r1 - r0, W]))
 
         nc.vector.memset(zero[:], 0.0)
-        shared_rows = unused[:, 14:16].rearrange("p r j -> p (r j)")
+        shared_rows = unused[:, shared_from : shared_from + 2].rearrange("p r j -> p (r j)")
         cut = 2 * W - SCALAR_ZEROS
         scalar_words = shared_rows[:, cut:].bitcast(U32)
         nc.scalar.mul(out=scalar_words, in_=scalar_words, mul=0.0)
-        nc.vector.memset(x_bf[TOP:P, 0:2].rearrange("p t c m u -> p (t c m u)").bitcast(U32), 0)
-        fill(0, 14)
-        fill(16, 20)
+        nc.vector.memset(x_bf[TOP:P, 0:EARLY].rearrange("p t c m u -> p (t c m u)").bitcast(U32), 0)
+        fill(0, shared_from)
+        fill(PACK * A_SLOT, PACK * (A_SLOT + 1))
         nc.vector.tensor_copy(
             out=shared_rows[:, 0:cut].rearrange("p (r j) -> p r j", r=2),
-            in_=zero[0:R, 0 : cut // 2].unsqueeze(1).to_broadcast([R, 2, cut // 2]),
+            in_=zero[:, 0 : cut // 2].unsqueeze(1).to_broadcast([R, 2, cut // 2]),
         )
 
         def deal_x(copy, c0, c1, t0):
@@ -109,6 +112,11 @@ def tile_rows_kron_sep_kernel(tc, x, a, b, cw, out):
         def quantise(codes, scales, values):
             nc.vector.quantize_mx(out=codes.bitcast(FP8X4), scales=scales, in_=values)
 
+        def quantise_half(t, c0):
+            cols = slice(R * c0, R * (c0 + 2))
+            values = x_bf[:, t, c0 : c0 + 2].rearrange("p c m u -> p (c m u)")
+            quantise(x_codes[:, t, cols], x_scales[:, t, cols], values)
+
         def product(sums, tile, codes, scales, moving_codes, moving_scales):
             rows = slice(R * tile, R * (tile + 1))
             nc.tensor.matmul_mx(
@@ -124,25 +132,21 @@ def tile_rows_kron_sep_kernel(tc, x, a, b, cw, out):
         vcopy = nc.vector.tensor_copy
         scopy = nc.scalar.copy
 
-        def quantise_half(t, c0):
-            cols = slice(R * c0, R * (c0 + 2))
-            quantise(x_codes[:, t, cols], x_scales[:, t, cols], x_bf[:, t, c0 : c0 + 2].rearrange("p c m u -> p (c m u)"))
-
         deal_x(vcopy, 0, 2, 0)
-        deal_x(scopy, 0, 1, 2)
+        deal_x(scopy, 0, 1, EARLY)
         interleave(scopy, a_bf[:], raw[:, A_SLOT], 0, SCALAR_SHARE)
         interleave(vcopy, a_bf[:], raw[:, A_SLOT], SCALAR_SHARE, R)
-        deal_x(scopy, 1, 2, 2)
+        deal_x(scopy, 1, 2, EARLY)
         deal_x(vcopy, 2, 3, 0)
-        deal_x(scopy, 2, 3, 2)
-        for t in range(2):
+        deal_x(scopy, 2, 3, EARLY)
+        for t in range(EARLY):
             quantise_half(t, 0)
         deal_x(vcopy, 3, 4, 0)
-        deal_x(scopy, 3, 4, 2)
+        deal_x(scopy, 3, 4, EARLY)
         quantise(a_codes[:], a_scales[:], a_bf[:].rearrange("p k u -> p (k u)"))
-        for t in range(2):
+        for t in range(EARLY):
             quantise_half(t, 2)
-        for t in range(2, PACK):
+        for t in range(EARLY, PACK):
             quantise(x_codes[0:TOP, t], x_scales[0:TOP, t], x_bf[0:TOP, t].rearrange("p c m u -> p (c m u)"))
 
         for t in range(PACK):
@@ -159,20 +163,9 @@ def tile_rows_kron_sep_kernel(tc, x, a, b, cw, out):
         for h in range(HALVES):
             quantise(z_codes[:, h], z_scales[:, h], z_bf[:, h].rearrange("p s q t -> p (s q t)"))
 
-        for c0, h in ((0, 0), (0, 1), (2, 0), (2, 1)):
-            for c in (c0, c0 + 1):
-                product(w_ps[c, h], c, z_codes[:, h], z_scales[:, h], b_codes, b_scales)
-
-        def weigh(c, h):
-            nc.vector.tensor_tensor(
-                out=res[:, c, h : h + 1],
-                in0=w_ps[c, h].unsqueeze(1),
-                in1=cw_sb[:, h : h + 1],
-                op=mybir.AluOpType.mult,
-            )
-
-        def weigh_both(c):
-            nc.vector.tensor_tensor(out=res[:, c], in0=w_pair[c][:], in1=cw_sb[:], op=mybir.AluOpType.mult)
+        order = [(c0 + i, h) for c0 in range(0, TILES, 2) for h in range(HALVES) for i in range(2)]
+        for c, h in order:
+            product(w_ps[c][h], c, z_codes[:, h], z_scales[:, h], b_codes, b_scales)
 
         def store(c, h0, h1):
             nc.sync.dma_start(
@@ -180,13 +173,9 @@ def tile_rows_kron_sep_kernel(tc, x, a, b, cw, out):
                 in_=res[:, c, h0:h1],
             )
 
-        weigh(0, 0)
-        store(0, 0, 1)
-        weigh(1, 0)
-        weigh(0, 1)
-        store(0, 1, 2)
-        weigh(1, 1)
-        store(1, 0, 2)
-        for c in range(2, TILES):
-            weigh_both(c)
-            store(c, 0, 2)
+        for c, h in order:
+            nc.vector.tensor_tensor(out=res[:, c, h], in0=w_ps[c][h], in1=cw_sb[:, h], op=mybir.AluOpType.mult)
+            if c == 0:
+                store(c, h, h + 1)
+            elif h == HALVES - 1:
+                store(c, 0, HALVES)

@@ -161,7 +161,9 @@ def tile_rows_kron_sep_kernel(tc, x, a, b, cw, out):
             for s, copy in enumerate((vcopy, scopy)):
                 copy(out=z_bf[:, h, s], in_=z_ps[s][:].rearrange("p t (q h) -> p h q t", h=HALVES)[:, h])
         for h in range(HALVES):
-            quantise(z_codes[:, h], z_scales[:, h], z_bf[:, h].rearrange("p s q t -> p (s q t)"))
+            for s in range(SETS):
+                cols = slice(PAIRS * s, PAIRS * (s + 1))
+                quantise(z_codes[:, h, cols], z_scales[:, h, cols], z_bf[:, h, s].rearrange("p q t -> p (q t)"))
 
         order = [(c0 + i, h) for c0 in range(0, TILES, 2) for h in range(HALVES) for i in range(2)]
         for c, h in order:

@@ -23,7 +23,7 @@ TOP = R + SETS * R
 A_SLOT = TILES
 EARLY = 2
 SCALAR_SHARE = 14
-SCALAR_ZEROS = 64
+SCALAR_ZEROS = 16
 
 
 def tile_rows_kron_sep_kernel(tc, x, a, b, cw, out):
@@ -89,7 +89,7 @@ def tile_rows_kron_sep_kernel(tc, x, a, b, cw, out):
         cut = 2 * W - SCALAR_ZEROS
         scalar_words = shared_rows[:, cut:].bitcast(U32)
         nc.scalar.mul(out=scalar_words, in_=scalar_words, mul=0.0)
-        nc.vector.memset(x_bf[TOP:P, 0:EARLY].rearrange("p t c m u -> p (t c m u)").bitcast(U32), 0)
+        nc.vector.memset(x_bf[TOP:P, 0].rearrange("p c m u -> p (c m u)").bitcast(U32), 0)
         fill(0, shared_from)
         fill(PACK * A_SLOT, PACK * (A_SLOT + 1))
         nc.vector.tensor_copy(
@@ -112,10 +112,10 @@ def tile_rows_kron_sep_kernel(tc, x, a, b, cw, out):
         def quantise(codes, scales, values):
             nc.vector.quantize_mx(out=codes.bitcast(FP8X4), scales=scales, in_=values)
 
-        def quantise_half(t, c0):
+        def quantise_half(c0):
             cols = slice(R * c0, R * (c0 + 2))
-            values = x_bf[:, t, c0 : c0 + 2].rearrange("p c m u -> p (c m u)")
-            quantise(x_codes[:, t, cols], x_scales[:, t, cols], values)
+            values = x_bf[:, 0, c0 : c0 + 2].rearrange("p c m u -> p (c m u)")
+            quantise(x_codes[:, 0, cols], x_scales[:, 0, cols], values)
 
         def product(sums, tile, codes, scales, moving_codes, moving_scales):
             rows = slice(R * tile, R * (tile + 1))
@@ -133,20 +133,18 @@ def tile_rows_kron_sep_kernel(tc, x, a, b, cw, out):
         scopy = nc.scalar.copy
 
         deal_x(vcopy, 0, 2, 0)
-        deal_x(scopy, 0, 1, EARLY)
+        deal_x(scopy, 1, 2, EARLY)
+        deal_x(vcopy, 0, 1, EARLY)
         interleave(scopy, a_bf[:], raw[:, A_SLOT], 0, SCALAR_SHARE)
         interleave(vcopy, a_bf[:], raw[:, A_SLOT], SCALAR_SHARE, R)
-        deal_x(scopy, 1, 2, EARLY)
         deal_x(vcopy, 2, 3, 0)
         deal_x(scopy, 2, 3, EARLY)
-        for t in range(EARLY):
-            quantise_half(t, 0)
+        quantise_half(0)
         deal_x(vcopy, 3, 4, 0)
         deal_x(scopy, 3, 4, EARLY)
         quantise(a_codes[:], a_scales[:], a_bf[:].rearrange("p k u -> p (k u)"))
-        for t in range(EARLY):
-            quantise_half(t, 2)
-        for t in range(EARLY, PACK):
+        quantise_half(2)
+        for t in range(1, PACK):
             quantise(x_codes[0:TOP, t], x_scales[0:TOP, t], x_bf[0:TOP, t].rearrange("p c m u -> p (c m u)"))
 
         for t in range(PACK):

@@ -14,16 +14,10 @@ FP8X4 = mybir.dt.float8_e4m3fn_x4
 P = 128
 R = 32
 PACK = 4
-SETS = 2
 TILES = 4
-HALVES = 2
-PAIRS = K // HALVES
+WAVES = 2
 W = 128
-TOP = R + SETS * R
-A_SLOT = TILES
-EARLY = 2
-SCALAR_SHARE = 14
-SCALAR_ZEROS = 16
+SCALAR_SHARE = 10
 
 
 def tile_rows_kron_sep_kernel(tc, x, a, b, cw, out):
@@ -33,149 +27,136 @@ def tile_rows_kron_sep_kernel(tc, x, a, b, cw, out):
         ps = ctx.enter_context(tc.psum_pool(name="ps", bufs=1))
         ctx.enter_context(tc.manual_schedule())
 
-        raw = sb.tile([TOP, TILES + 1, PACK, W], F32, name="raw", align_bytes=64)
-        cw_sb = sb.tile([P, HALVES, L], F32, name="cw_sb", align_bytes=64)
-        x_bf = sb.tile([P, PACK, TILES, R, PACK], BF16, name="x_bf", align_bytes=64)
-        a_bf = sb.tile([TOP, K, PACK], BF16, name="a_bf", align_bytes=64)
-        b_raw = sb.tile([P, PACK, L], F32, name="b_raw", align_bytes=64)
-        b_bf = sb.tile([P, L, PACK], BF16, name="b_bf", align_bytes=64)
-        z_bf = sb.tile([P, HALVES, SETS, PAIRS, PACK], BF16, name="z_bf", align_bytes=64)
-        x_codes = sb.tile([P, PACK, W], U32, name="x_codes", align_bytes=64)
-        x_scales = sb.tile([P, PACK, W], U8, name="x_scales", align_bytes=64)
-        a_codes = sb.tile([TOP, W], U32, name="a_codes", align_bytes=64)
-        a_scales = sb.tile([TOP, W], U8, name="a_scales", align_bytes=64)
-        b_codes = sb.tile([P, W], U32, name="b_codes", align_bytes=64)
-        b_scales = sb.tile([P, W], U8, name="b_scales", align_bytes=64)
-        z_codes = sb.tile([P, HALVES, W], U32, name="z_codes", align_bytes=64)
-        z_scales = sb.tile([P, HALVES, W], U8, name="z_scales", align_bytes=64)
-        res = sb.tile([P, TILES, HALVES, L], F32, name="res", align_bytes=64)
-        zero = sb.tile([R, W], F32, name="zero", align_bytes=64)
+        def tile(shape, dtype, name):
+            return sb.tile(shape, dtype, name=name, align_bytes=64)
 
-        z_ps = [ps.tile([P, PACK, K], F32, name="z_ps%d" % s) for s in range(SETS)]
-        w_even = [ps.tile([P, L], F32, name="w_even%d" % c) for c in range(TILES)]
-        w_odd_first = ps.tile([P, L], F32, name="w_odd_first")
-        w_odd_last = ps.tile([P, L], F32, name="w_odd_last")
-        w_odd = [w_odd_first[:], z_ps[0][:, 0], z_ps[1][:, 0], w_odd_last[:]]
-        w_ps = [[w_even[c][:], w_odd[c]] for c in range(TILES)]
+        a_raw = tile([P, PACK, K], F32, "a_raw")
+        b_raw = tile([P, PACK, L], F32, "b_raw")
+        x_raw = [tile([P, PACK, J], F32, "x_raw%d" % v) for v in range(WAVES)]
+        cw_sb = tile([P, TILES, L], F32, "cw_sb")
+        a_bf = tile([P, TILES, R, PACK], BF16, "a_bf")
+        b_bf = tile([P, L, PACK], BF16, "b_bf")
+        x_bf = [tile([P, PACK, R, PACK], BF16, "x_bf%d" % v) for v in range(WAVES)]
+        z_t = [[tile([P, 2, PACK, R], F32, "z_t%d%d" % (v, i)) for i in range(2)] for v in range(WAVES)]
+        z_bf = [tile([P, TILES, R, PACK], BF16, "z_bf%d" % v) for v in range(WAVES)]
+        res = [tile([P, TILES, L], F32, "res%d" % v) for v in range(WAVES)]
 
-        a_rows = a.rearrange("(p u) k -> p u k", u=PACK)
-        b_rows = b.rearrange("(p t) l -> p t l", t=PACK)
-        cw_rows = cw.rearrange("(q h) l -> q h l", h=HALVES)
+        def operand(name):
+            return tile([P, W], U32, name + "_codes"), tile([P, W], U8, name + "_scales")
 
-        def load_x(c0, c1):
-            nc.sync.dma_start(
-                out=raw[R:TOP, c0:c1].rearrange("p c u j -> p c (u j)"),
-                in_=x.rearrange("(c s) (p u) j -> (s p) c (u j)", s=SETS, u=PACK)[:, c0:c1],
-            )
+        a_mx = operand("a")
+        b_mx = operand("b")
+        x_mx = [operand("x%d" % v) for v in range(WAVES)]
+        z_mx = [operand("z%d" % v) for v in range(WAVES)]
+        bank = [[ps.tile([P, W], F32, name="bank%d%d" % (v, r)) for r in range(TILES)] for v in range(WAVES)]
 
-        load_x(0, 2)
-        for s in range(SETS):
-            nc.sync.dma_start(out=raw[R * (s + 1) : R * (s + 2), A_SLOT], in_=a_rows)
-        for c in range(2, TILES):
-            load_x(c, c + 1)
-        for c in (0, 2, 1, 3):
-            nc.sync.dma_start(out=b_raw[R * c : R * (c + 1)], in_=b_rows)
-        for s in range(SETS):
-            nc.sync.dma_start(out=cw_sb[PAIRS * s : PAIRS * (s + 1)], in_=cw_rows)
+        def spread(dst, src):
+            rows = src.rearrange("(p u) n -> p u n", u=PACK)
+            for r in (0, 2, 1, 3):
+                nc.sync.dma_start(out=dst[R * r : R * (r + 1)], in_=rows)
 
-        unused = raw[0:R].rearrange("p c u j -> p (c u) j")
-        shared_from = PACK * TILES - 2
+        def matrices(t, v):
+            return t[TILES * v : TILES * (v + 1)].rearrange("r (p u) n -> (r p) u n", u=PACK)
 
-        def fill(r0, r1):
-            nc.vector.tensor_copy(out=unused[:, r0:r1], in_=zero[:].unsqueeze(1).to_broadcast([R, r1 - r0, W]))
+        spread(a_raw, a)
+        for v in range(WAVES):
+            nc.sync.dma_start(out=x_raw[v][:], in_=matrices(x, v))
+        spread(b_raw, b)
+        spread(cw_sb, cw)
 
-        nc.vector.memset(zero[:], 0.0)
-        shared_rows = unused[:, shared_from : shared_from + 2].rearrange("p r j -> p (r j)")
-        cut = 2 * W - SCALAR_ZEROS
-        scalar_words = shared_rows[:, cut:].bitcast(U32)
-        nc.scalar.mul(out=scalar_words, in_=scalar_words, mul=0.0)
-        nc.vector.memset(x_bf[TOP:P, 0].rearrange("p c m u -> p (c m u)").bitcast(U32), 0)
-        fill(0, shared_from)
-        fill(PACK * A_SLOT, PACK * (A_SLOT + 1))
-        nc.vector.tensor_copy(
-            out=shared_rows[:, 0:cut].rearrange("p (r j) -> p r j", r=2),
-            in_=zero[:, 0 : cut // 2].unsqueeze(1).to_broadcast([R, 2, cut // 2]),
-        )
-
-        def deal_x(copy, c0, c1, t0):
-            copy(
-                out=x_bf[0:TOP, t0 : t0 + 2, c0:c1].rearrange("p t c m u -> p c m u t"),
-                in_=raw[:, c0:c1].rearrange("p c u (m t) -> p c m u t", t=PACK)[:, :, :, :, t0 : t0 + 2],
-            )
-
-        def interleave(copy, dst, src, n0, n1):
-            copy(
-                out=dst.rearrange("p (n i) u -> p n u i", i=PACK)[:, n0:n1],
-                in_=src.rearrange("p u (n i) -> p n u i", i=PACK)[:, n0:n1],
-            )
-
-        def quantise(codes, scales, values):
-            nc.vector.quantize_mx(out=codes.bitcast(FP8X4), scales=scales, in_=values)
-
-        def quantise_half(c0):
-            cols = slice(R * c0, R * (c0 + 2))
-            values = x_bf[:, 0, c0 : c0 + 2].rearrange("p c m u -> p (c m u)")
-            quantise(x_codes[:, 0, cols], x_scales[:, 0, cols], values)
-
-        def product(sums, tile, codes, scales, moving_codes, moving_scales):
-            rows = slice(R * tile, R * (tile + 1))
-            nc.tensor.matmul_mx(
-                out=sums,
-                lhsT=codes[rows].bitcast(FP8X4),
-                lhsT_scale=scales[rows],
-                rhs=moving_codes[rows].bitcast(FP8X4),
-                rhs_scale=moving_scales[rows],
-                start=True,
-                stop=True,
-            )
+        warm = tile([R, 1], U32, "warm")
+        nc.scalar.mul(out=warm[:], in_=warm[:], mul=0.0)
 
         vcopy = nc.vector.tensor_copy
         scopy = nc.scalar.copy
 
-        deal_x(vcopy, 0, 2, 0)
-        deal_x(scopy, 1, 2, EARLY)
-        deal_x(vcopy, 0, 1, EARLY)
-        interleave(scopy, a_bf[:], raw[:, A_SLOT], 0, SCALAR_SHARE)
-        interleave(vcopy, a_bf[:], raw[:, A_SLOT], SCALAR_SHARE, R)
-        deal_x(vcopy, 2, 3, 0)
-        deal_x(scopy, 2, 3, EARLY)
-        quantise_half(0)
-        deal_x(vcopy, 3, 4, 0)
-        deal_x(scopy, 3, 4, EARLY)
-        quantise(a_codes[:], a_scales[:], a_bf[:].rearrange("p k u -> p (k u)"))
-        quantise_half(2)
-        for t in range(1, PACK):
-            quantise(x_codes[0:TOP, t], x_scales[0:TOP, t], x_bf[0:TOP, t].rearrange("p c m u -> p (c m u)"))
-
-        for t in range(PACK):
-            for s in range(SETS):
-                product(z_ps[s][:, t], s + 1, x_codes[:, t], x_scales[:, t], a_codes, a_scales)
-
-        interleave(scopy, b_bf[:], b_raw[:], 0, SCALAR_SHARE)
-        interleave(vcopy, b_bf[:], b_raw[:], SCALAR_SHARE, R)
-        quantise(b_codes[:], b_scales[:], b_bf[:].rearrange("p l t -> p (l t)"))
-
-        for h in range(HALVES):
-            for s, copy in enumerate((vcopy, scopy)):
-                copy(out=z_bf[:, h, s], in_=z_ps[s][:].rearrange("p t (q h) -> p h q t", h=HALVES)[:, h])
-        for h in range(HALVES):
-            for s in range(SETS):
-                cols = slice(PAIRS * s, PAIRS * (s + 1))
-                quantise(z_codes[:, h, cols], z_scales[:, h, cols], z_bf[:, h, s].rearrange("p q t -> p (q t)"))
-
-        order = [(c0 + i, h) for c0 in range(0, TILES, 2) for h in range(HALVES) for i in range(2)]
-        for c, h in order:
-            product(w_ps[c][h], c, z_codes[:, h], z_scales[:, h], b_codes, b_scales)
-
-        def store(c, h0, h1):
-            nc.sync.dma_start(
-                out=out[SETS * c : SETS * (c + 1)].rearrange("s (q h) l -> (s q) h l", h=HALVES)[:, h0:h1],
-                in_=res[:, c, h0:h1],
+        def deal(copy, dst, src, m0, m1):
+            copy(
+                out=dst.rearrange("p t m u -> p m u t")[:, m0:m1],
+                in_=src.rearrange("p u (m t) -> p m u t", t=PACK)[:, m0:m1],
             )
 
-        for c, h in order:
-            nc.vector.tensor_tensor(out=res[:, c, h], in0=w_ps[c][h], in1=cw_sb[:, h], op=mybir.AluOpType.mult)
-            if c == 0:
-                store(c, h, h + 1)
-            elif h == HALVES - 1:
-                store(c, 0, HALVES)
+        def quantise(mx, values):
+            nc.vector.quantize_mx(out=mx[0][:].bitcast(FP8X4), scales=mx[1][:], in_=values)
+
+        def flat(t):
+            return t[:].rearrange("p a b c -> p (a b c)")
+
+        def product(sums, r, stationary, moving):
+            rows = slice(R * r, R * (r + 1))
+            nc.tensor.matmul_mx(
+                out=sums,
+                lhsT=stationary[0][rows].bitcast(FP8X4),
+                lhsT_scale=stationary[1][rows],
+                rhs=moving[0][rows].bitcast(FP8X4),
+                rhs_scale=moving[1][rows],
+                start=True,
+                stop=True,
+            )
+
+        def first(v):
+            for r in range(TILES):
+                product(bank[v][r][:], r, a_mx, x_mx[v])
+
+        def turn(v, r):
+            nc.vector.transpose(out=z_t[v][r // 2][:, r % 2].rearrange("p t q -> p (t q)"), in_=bank[v][r][:])
+
+        def round_z(copy, v, r0, r1):
+            copy(
+                out=z_bf[v][:, r0:r1].rearrange("p r (n e) t -> p r n t e", e=PACK),
+                in_=z_t[v][r0 // 2][:, r0 % 2 : r0 % 2 + r1 - r0].rearrange("p r t (n e) -> p r n t e", e=PACK),
+            )
+
+        def quantise_pair(v, r0):
+            cols = slice(R * r0, R * (r0 + 2))
+            nc.vector.quantize_mx(
+                out=z_mx[v][0][:, cols].bitcast(FP8X4),
+                scales=z_mx[v][1][:, cols],
+                in_=z_bf[v][:, r0 : r0 + 2].rearrange("p a b c -> p (a b c)"),
+            )
+
+        def second(v):
+            for c in range(TILES):
+                product(bank[v][c][:], c, z_mx[v], b_mx)
+
+        def weigh(v, c):
+            nc.vector.tensor_tensor(out=res[v][:, c], in0=bank[v][c][:], in1=cw_sb[:, c], op=mybir.AluOpType.mult)
+            if c % 2 == 1:
+                nc.sync.dma_start(out=matrices(out, v)[:, c - 1 : c + 1], in_=res[v][:, c - 1 : c + 1])
+
+        deal(scopy, a_bf[:], a_raw[:], 0, SCALAR_SHARE)
+        deal(vcopy, a_bf[:], a_raw[:], SCALAR_SHARE, R)
+        deal(scopy, x_bf[0][:], x_raw[0][:], 0, SCALAR_SHARE)
+        deal(vcopy, x_bf[0][:], x_raw[0][:], SCALAR_SHARE, R)
+        quantise(a_mx, flat(a_bf))
+        quantise(x_mx[0], flat(x_bf[0]))
+        first(0)
+        deal(scopy, x_bf[1][:], x_raw[1][:], 0, SCALAR_SHARE)
+        deal(vcopy, x_bf[1][:], x_raw[1][:], SCALAR_SHARE, R)
+        quantise(x_mx[1], flat(x_bf[1]))
+        first(1)
+        nc.gpsimd.tensor_scalar(
+            out=b_bf[:],
+            in0=b_raw[:].rearrange("p t l -> p l t"),
+            scalar1=1.0,
+            scalar2=0.0,
+            op0=mybir.AluOpType.mult,
+            op1=mybir.AluOpType.add,
+        )
+        for r in range(TILES):
+            turn(0, r)
+            round_z(scopy, 0, r, r + 1)
+        for r in range(TILES):
+            turn(1, r)
+        round_z(scopy, 1, 0, 2)
+        round_z(scopy, 1, 2, 3)
+        quantise(b_mx, b_bf[:].rearrange("p l t -> p (l t)"))
+        quantise(z_mx[0], flat(z_bf[0]))
+        second(0)
+        round_z(vcopy, 1, 3, 4)
+        quantise_pair(1, 0)
+        quantise_pair(1, 2)
+        second(1)
+        for v in range(WAVES):
+            for c in range(TILES):
+                weigh(v, c)

@@ -16,8 +16,14 @@ R = 32
 PACK = 4
 TILES = 4
 WAVES = 2
+SETS = 2
+SLOTS = 4
 W = 128
-SCALAR_SHARE = 10
+TOP = R + SETS * R
+SCALAR_SHARE = 14
+ZEROS = 8
+HALF = 64
+CLASS_OF_TILE = (2, 0, 1, 3)
 
 
 def tile_rows_kron_sep_kernel(tc, x, a, b, cw, out):
@@ -30,57 +36,75 @@ def tile_rows_kron_sep_kernel(tc, x, a, b, cw, out):
         def tile(shape, dtype, name):
             return sb.tile(shape, dtype, name=name, align_bytes=64)
 
-        a_raw = tile([P, PACK, K], F32, "a_raw")
+        raw = tile([TOP, 1 + SLOTS, PACK, W], F32, "raw")
         b_raw = tile([P, PACK, L], F32, "b_raw")
-        x_raw = [tile([P, PACK, J], F32, "x_raw%d" % v) for v in range(WAVES)]
         cw_sb = tile([P, TILES, L], F32, "cw_sb")
-        a_bf = tile([P, TILES, R, PACK], BF16, "a_bf")
+        a_bf = tile([TOP, TILES, R, PACK], BF16, "a_bf")
         b_bf = tile([P, L, PACK], BF16, "b_bf")
-        x_bf = [tile([P, PACK, R, PACK], BF16, "x_bf%d" % v) for v in range(WAVES)]
-        z_t = [[tile([P, 2, PACK, R], F32, "z_t%d%d" % (v, i)) for i in range(2)] for v in range(WAVES)]
-        z_bf = [tile([P, TILES, R, PACK], BF16, "z_bf%d" % v) for v in range(WAVES)]
+        x_bf = [tile([TOP, PACK, R, PACK], BF16, "x_bf%d" % n) for n in range(SLOTS)]
+        z_t = [tile([P, SETS, PACK, R], F32, "z_t%d" % n) for n in range(SLOTS)]
+        z_bf = [tile([P, R, TILES, PACK], BF16, "z_bf%d" % v) for v in range(WAVES)]
         res = [tile([P, TILES, L], F32, "res%d" % v) for v in range(WAVES)]
+        zero = tile([R, ZEROS], F32, "zero")
 
-        def operand(name):
-            return tile([P, W], U32, name + "_codes"), tile([P, W], U8, name + "_scales")
+        def operand(parts, name):
+            return tile([parts, W], U32, name + "_codes"), tile([parts, W], U8, name + "_scales")
 
-        a_mx = operand("a")
-        b_mx = operand("b")
-        x_mx = [operand("x%d" % v) for v in range(WAVES)]
-        z_mx = [operand("z%d" % v) for v in range(WAVES)]
-        bank = [[ps.tile([P, W], F32, name="bank%d%d" % (v, r)) for r in range(TILES)] for v in range(WAVES)]
+        a_mx = operand(TOP, "a")
+        b_mx = operand(P, "b")
+        x_mx = [operand(TOP, "x%d" % n) for n in range(SLOTS)]
+        z_mx = [operand(P, "z%d" % v) for v in range(WAVES)]
+        inner = [[ps.tile([P, W], F32, name="inner%d%d" % (s, i)) for i in range(3)] for s in range(SETS)]
+        outer = [ps.tile([P, W], F32, name="outer%d" % i) for i in range(2)]
+        w_bank = [[outer[0], inner[0][1 + v], inner[1][1 + v], outer[1]] for v in range(WAVES)]
 
-        def spread(dst, src):
+        def spread(dst, src, tiles):
             rows = src.rearrange("(p u) n -> p u n", u=PACK)
-            for r in (0, 2, 1, 3):
+            for r in tiles:
                 nc.sync.dma_start(out=dst[R * r : R * (r + 1)], in_=rows)
 
-        def matrices(t, v):
-            return t[TILES * v : TILES * (v + 1)].rearrange("r (p u) n -> (r p) u n", u=PACK)
+        def matrices(t, g0, g1):
+            return t[g0:g1].rearrange("r (p u) n -> (r p) u n", u=PACK)
 
-        spread(a_raw, a)
-        for v in range(WAVES):
-            nc.sync.dma_start(out=x_raw[v][:], in_=matrices(x, v))
-        spread(b_raw, b)
-        spread(cw_sb, cw)
+        spread(raw[:, 0], a, (1, 2))
+        for n in range(SLOTS):
+            nc.sync.dma_start(out=raw[R:TOP, 1 + n], in_=matrices(x, SETS * n, SETS * (n + 1)))
+        spread(b_raw, b, (0, 2, 1, 3))
+        nc.sync.dma_start(
+            out=cw_sb[:].rearrange("p c l -> p (c l)"),
+            in_=cw.rearrange("(q c) l -> q (c l)", c=TILES).unsqueeze(1).to_broadcast([R, TILES, TILES * L]),
+        )
 
-        warm = tile([R, 1], U32, "warm")
-        nc.scalar.mul(out=warm[:], in_=warm[:], mul=0.0)
+        unused = raw[0:R].rearrange("p c u (n j) -> p (c u n) j", j=ZEROS)
+        last = unused.shape[1] - 2
+        nc.vector.memset(zero[:], 0.0)
+        scalar_words = unused[:, last:].rearrange("p n j -> p (n j)").bitcast(U32)
+        nc.scalar.mul(out=scalar_words, in_=scalar_words, mul=0.0)
+        nc.vector.tensor_copy(out=unused[:, 0:last], in_=zero[:].unsqueeze(1).to_broadcast([R, last, ZEROS]))
 
         vcopy = nc.vector.tensor_copy
         scopy = nc.scalar.copy
 
-        def deal(copy, dst, src, m0, m1):
+        def deal(copy, n, m0, m1):
             copy(
-                out=dst.rearrange("p t m u -> p m u t")[:, m0:m1],
-                in_=src.rearrange("p u (m t) -> p m u t", t=PACK)[:, m0:m1],
+                out=x_bf[n][:].rearrange("p t m u -> p m u t")[:, m0:m1],
+                in_=raw[:, 1 + n].rearrange("p u (m t) -> p m u t", t=PACK)[:, m0:m1],
             )
 
-        def quantise(mx, values):
-            nc.vector.quantize_mx(out=mx[0][:].bitcast(FP8X4), scales=mx[1][:], in_=values)
+        def deal_shared(n):
+            deal(scopy, n, 0, SCALAR_SHARE)
+            deal(vcopy, n, SCALAR_SHARE, R)
 
-        def flat(t):
-            return t[:].rearrange("p a b c -> p (a b c)")
+        def deal_a(copy, blocks, t0):
+            copy(
+                out=a_bf[:, blocks].rearrange("p c q u -> p q u c"),
+                in_=raw[:, 0].rearrange("p u (q t) -> p q u t", t=PACK)[:, :, :, t0 : t0 + 2],
+            )
+
+        def quantise(mx, values, cols=slice(0, W)):
+            nc.vector.quantize_mx(
+                out=mx[0][:, cols].bitcast(FP8X4), scales=mx[1][:, cols], in_=values.rearrange("p a b c -> p (a b c)")
+            )
 
         def product(sums, r, stationary, moving):
             rows = slice(R * r, R * (r + 1))
@@ -94,69 +118,87 @@ def tile_rows_kron_sep_kernel(tc, x, a, b, cw, out):
                 stop=True,
             )
 
-        def first(v):
-            for r in range(TILES):
-                product(bank[v][r][:], r, a_mx, x_mx[v])
+        def passes(n):
+            for s in range(SETS):
+                product(inner[s][n % 3][:], 1 + s, a_mx, x_mx[n])
 
-        def turn(v, r):
-            nc.vector.transpose(out=z_t[v][r // 2][:, r % 2].rearrange("p t q -> p (t q)"), in_=bank[v][r][:])
+        def first(n):
+            quantise(x_mx[n], x_bf[n][:])
+            passes(n)
 
-        def round_z(copy, v, r0, r1):
+        def turn(n, s):
+            nc.vector.transpose(out=z_t[n][:, s].rearrange("p t q -> p (t q)"), in_=inner[s][n % 3][:])
+
+        def round_z(copy, n, n0, n1):
+            r0 = SETS * (n % 2)
             copy(
-                out=z_bf[v][:, r0:r1].rearrange("p r (n e) t -> p r n t e", e=PACK),
-                in_=z_t[v][r0 // 2][:, r0 % 2 : r0 % 2 + r1 - r0].rearrange("p r t (n e) -> p r n t e", e=PACK),
+                out=z_bf[n // 2][:, :, r0 : r0 + SETS].rearrange("p (n e) r t -> p n (r t) e", e=PACK)[:, n0:n1],
+                in_=z_t[n][:].rearrange("p r t (n e) -> p n (r t) e", e=PACK)[:, n0:n1],
             )
 
-        def quantise_pair(v, r0):
-            cols = slice(R * r0, R * (r0 + 2))
-            nc.vector.quantize_mx(
-                out=z_mx[v][0][:, cols].bitcast(FP8X4),
-                scales=z_mx[v][1][:, cols],
-                in_=z_bf[v][:, r0 : r0 + 2].rearrange("p a b c -> p (a b c)"),
-            )
+        order = ((0, 3, 1, 2), (1, 2, 0, 3))
 
-        def second(v):
-            for c in range(TILES):
-                product(bank[v][c][:], c, z_mx[v], b_mx)
+        def second(v, tiles):
+            for c in tiles:
+                product(w_bank[v][c][:], c, z_mx[v], b_mx)
 
         def weigh(v, c):
-            nc.vector.tensor_tensor(out=res[v][:, c], in0=bank[v][c][:], in1=cw_sb[:, c], op=mybir.AluOpType.mult)
-            if c % 2 == 1:
-                nc.sync.dma_start(out=matrices(out, v)[:, c - 1 : c + 1], in_=res[v][:, c - 1 : c + 1])
+            k = CLASS_OF_TILE[c]
+            nc.vector.tensor_tensor(out=res[v][:, k], in0=w_bank[v][c][:], in1=cw_sb[:, k], op=mybir.AluOpType.mult)
 
-        deal(scopy, a_bf[:], a_raw[:], 0, SCALAR_SHARE)
-        deal(vcopy, a_bf[:], a_raw[:], SCALAR_SHARE, R)
-        deal(scopy, x_bf[0][:], x_raw[0][:], 0, SCALAR_SHARE)
-        deal(vcopy, x_bf[0][:], x_raw[0][:], SCALAR_SHARE, R)
-        quantise(a_mx, flat(a_bf))
-        quantise(x_mx[0], flat(x_bf[0]))
-        first(0)
-        deal(scopy, x_bf[1][:], x_raw[1][:], 0, SCALAR_SHARE)
-        deal(vcopy, x_bf[1][:], x_raw[1][:], SCALAR_SHARE, R)
-        quantise(x_mx[1], flat(x_bf[1]))
-        first(1)
+        def store(v, k0, k1):
+            rows = out[TILES * v : TILES * (v + 1)].rearrange("r (q c) l -> q r (c l)", c=TILES)
+            nc.sync.dma_start(out=rows[:, :, L * k0 : L * k1], in_=res[v][:, k0:k1].rearrange("p c l -> p (c l)"))
+
+        def finish(v, i0, i1):
+            for i in range(i0, i1):
+                c = order[v][i]
+                weigh(v, c)
+                k = CLASS_OF_TILE[c]
+                if v == 0 and i < 2:
+                    store(v, k, k + 1)
+                elif i % 2 == 1:
+                    store(v, k - 1, k + 1)
+
+        deal_a(vcopy, slice(1, 3), 0)
+        deal_a(scopy, slice(0, 4, 3), 2)
+        deal_shared(0)
+        quantise(a_mx, a_bf[:])
+        for n in range(1, SLOTS):
+            deal_shared(n)
+            first(n - 1)
+        turn(0, 0)
+        quantise(x_mx[3], x_bf[3][:])
+        turn(0, 1)
+        passes(3)
         nc.gpsimd.tensor_scalar(
-            out=b_bf[:],
-            in0=b_raw[:].rearrange("p t l -> p l t"),
+            out=b_bf[:, 0:HALF],
+            in0=b_raw[:].rearrange("p t l -> p l t")[:, 0:HALF],
             scalar1=1.0,
             scalar2=0.0,
             op0=mybir.AluOpType.mult,
             op1=mybir.AluOpType.add,
         )
-        for r in range(TILES):
-            turn(0, r)
-            round_z(scopy, 0, r, r + 1)
-        for r in range(TILES):
-            turn(1, r)
-        round_z(scopy, 1, 0, 2)
-        round_z(scopy, 1, 2, 3)
-        quantise(b_mx, b_bf[:].rearrange("p l t -> p (l t)"))
-        quantise(z_mx[0], flat(z_bf[0]))
-        second(0)
-        round_z(vcopy, 1, 3, 4)
-        quantise_pair(1, 0)
-        quantise_pair(1, 2)
-        second(1)
-        for v in range(WAVES):
-            for c in range(TILES):
-                weigh(v, c)
+        scopy(
+            out=b_bf[:, HALF:].rearrange("p (n i) u -> p n u i", i=PACK),
+            in_=b_raw[:, :, HALF:].rearrange("p u (n i) -> p n u i", i=PACK),
+        )
+        round_z(scopy, 0, 0, 8)
+        turn(1, 0)
+        turn(1, 1)
+        round_z(scopy, 1, 0, 8)
+        turn(2, 0)
+        turn(2, 1)
+        round_z(scopy, 2, 0, 8)
+        turn(3, 0)
+        turn(3, 1)
+        round_z(scopy, 3, 0, 2)
+        quantise(b_mx, b_bf[:].unsqueeze(1))
+        quantise(z_mx[0], z_bf[0][:])
+        second(0, order[0])
+        round_z(vcopy, 3, 2, 8)
+        quantise(z_mx[1], z_bf[1][:])
+        finish(0, 0, 2)
+        second(1, order[1])
+        finish(0, 2, 4)
+        finish(1, 0, 4)

@@ -20,7 +20,7 @@ SETS = 2
 SLOTS = 4
 W = 128
 TOP = R + SETS * R
-SCALAR_SHARE = 14
+SCALAR_SHARE = 16
 ZEROS = 8
 HALF = 64
 CLASS_OF_TILE = (2, 0, 1, 3)
@@ -192,11 +192,11 @@ def tile_rows_kron_sep_kernel(tc, x, a, b, cw, out):
         round_z(scopy, 2, 0, 8)
         turn(3, 0)
         turn(3, 1)
-        round_z(scopy, 3, 0, 2)
+        round_z(scopy, 3, 0, 4)
         quantise(b_mx, b_bf[:].unsqueeze(1))
         quantise(z_mx[0], z_bf[0][:])
         second(0, order[0])
-        round_z(vcopy, 3, 2, 8)
+        round_z(vcopy, 3, 4, 8)
         quantise(z_mx[1], z_bf[1][:])
         finish(0, 0, 2)
         second(1, order[1])

from contextlib import ExitStack

import concourse.mybir as mybir

G, D, J, K, L = 8, 128, 128, 128, 128
FLOPS = 2 * G * (D * J * K + J * K * L)

F32 = mybir.dt.float32
BF16 = mybir.dt.bfloat16
U32 = mybir.dt.uint32
U8 = mybir.dt.uint8
FP8X4 = mybir.dt.float8_e4m3fn_x4

P = 128
R = 32
PACK = 4
TILES = 4
WAVES = 2
SETS = 2
SLOTS = 4
W = 128
TOP = R + SETS * R
SCALAR_SHARE = 16
ZEROS = 8
HALF = 64
CLASS_OF_TILE = (2, 0, 1, 3)


def tile_rows_kron_sep_kernel(tc, x, a, b, cw, out):
    nc = tc.nc
    with ExitStack() as ctx:
        sb = ctx.enter_context(tc.tile_pool(name="sb", bufs=1))
        ps = ctx.enter_context(tc.psum_pool(name="ps", bufs=1))
        ctx.enter_context(tc.manual_schedule())

        def tile(shape, dtype, name):
            return sb.tile(shape, dtype, name=name, align_bytes=64)

        raw = tile([TOP, 1 + SLOTS, PACK, W], F32, "raw")
        b_raw = tile([P, PACK, L], F32, "b_raw")
        cw_sb = tile([P, TILES, L], F32, "cw_sb")
        a_bf = tile([TOP, TILES, R, PACK], BF16, "a_bf")
        b_bf = tile([P, L, PACK], BF16, "b_bf")
        x_bf = [tile([TOP, PACK, R, PACK], BF16, "x_bf%d" % n) for n in range(SLOTS)]
        z_t = [tile([P, SETS, PACK, R], F32, "z_t%d" % n) for n in range(SLOTS)]
        z_bf = [tile([P, R, TILES, PACK], BF16, "z_bf%d" % v) for v in range(WAVES)]
        res = [tile([P, TILES, L], F32, "res%d" % v) for v in range(WAVES)]
        zero = tile([R, ZEROS], F32, "zero")

        def operand(parts, name):
            return tile([parts, W], U32, name + "_codes"), tile([parts, W], U8, name + "_scales")

        a_mx = operand(TOP, "a")
        b_mx = operand(P, "b")
        x_mx = [operand(TOP, "x%d" % n) for n in range(SLOTS)]
        z_mx = [operand(P, "z%d" % v) for v in range(WAVES)]
        inner = [[ps.tile([P, W], F32, name="inner%d%d" % (s, i)) for i in range(3)] for s in range(SETS)]
        outer = [ps.tile([P, W], F32, name="outer%d" % i) for i in range(2)]
        w_bank = [[outer[0], inner[0][1 + v], inner[1][1 + v], outer[1]] for v in range(WAVES)]

        def spread(dst, src, tiles):
            rows = src.rearrange("(p u) n -> p u n", u=PACK)
            for r in tiles:
                nc.sync.dma_start(out=dst[R * r : R * (r + 1)], in_=rows)

        def matrices(t, g0, g1):
            return t[g0:g1].rearrange("r (p u) n -> (r p) u n", u=PACK)

        spread(raw[:, 0], a, (1, 2))
        for n in range(SLOTS):
            nc.sync.dma_start(out=raw[R:TOP, 1 + n], in_=matrices(x, SETS * n, SETS * (n + 1)))
        spread(b_raw, b, (0, 2, 1, 3))
        nc.sync.dma_start(
            out=cw_sb[:].rearrange("p c l -> p (c l)"),
            in_=cw.rearrange("(q c) l -> q (c l)", c=TILES).unsqueeze(1).to_broadcast([R, TILES, TILES * L]),
        )

        unused = raw[0:R].rearrange("p c u (n j) -> p (c u n) j", j=ZEROS)
        last = unused.shape[1] - 2
        nc.vector.memset(zero[:], 0.0)
        scalar_words = unused[:, last:].rearrange("p n j -> p (n j)").bitcast(U32)
        nc.scalar.mul(out=scalar_words, in_=scalar_words, mul=0.0)
        nc.vector.tensor_copy(out=unused[:, 0:last], in_=zero[:].unsqueeze(1).to_broadcast([R, last, ZEROS]))

        vcopy = nc.vector.tensor_copy
        scopy = nc.scalar.copy

        def deal(copy, n, m0, m1):
            copy(
                out=x_bf[n][:].rearrange("p t m u -> p m u t")[:, m0:m1],
                in_=raw[:, 1 + n].rearrange("p u (m t) -> p m u t", t=PACK)[:, m0:m1],
            )

        def deal_shared(n):
            deal(scopy, n, 0, SCALAR_SHARE)
            deal(vcopy, n, SCALAR_SHARE, R)

        def deal_a(copy, blocks, t0):
            copy(
                out=a_bf[:, blocks].rearrange("p c q u -> p q u c"),
                in_=raw[:, 0].rearrange("p u (q t) -> p q u t", t=PACK)[:, :, :, t0 : t0 + 2],
            )

        def quantise(mx, values, cols=slice(0, W)):
            nc.vector.quantize_mx(
                out=mx[0][:, cols].bitcast(FP8X4), scales=mx[1][:, cols], in_=values.rearrange("p a b c -> p (a b c)")
            )

        def product(sums, r, stationary, moving):
            rows = slice(R * r, R * (r + 1))
            nc.tensor.matmul_mx(
                out=sums,
                lhsT=stationary[0][rows].bitcast(FP8X4),
                lhsT_scale=stationary[1][rows],
                rhs=moving[0][rows].bitcast(FP8X4),
                rhs_scale=moving[1][rows],
                start=True,
                stop=True,
            )

        def passes(n):
            for s in range(SETS):
                product(inner[s][n % 3][:], 1 + s, a_mx, x_mx[n])

        def first(n):
            quantise(x_mx[n], x_bf[n][:])
            passes(n)

        def turn(n, s):
            nc.vector.transpose(out=z_t[n][:, s].rearrange("p t q -> p (t q)"), in_=inner[s][n % 3][:])

        def round_z(copy, n, n0, n1):
            r0 = SETS * (n % 2)
            copy(
                out=z_bf[n // 2][:, :, r0 : r0 + SETS].rearrange("p (n e) r t -> p n (r t) e", e=PACK)[:, n0:n1],
                in_=z_t[n][:].rearrange("p r t (n e) -> p n (r t) e", e=PACK)[:, n0:n1],
            )

        order = ((0, 3, 1, 2), (1, 2, 0, 3))

        def second(v, tiles):
            for c in tiles:
                product(w_bank[v][c][:], c, z_mx[v], b_mx)

        def weigh(v, c):
            k = CLASS_OF_TILE[c]
            nc.vector.tensor_tensor(out=res[v][:, k], in0=w_bank[v][c][:], in1=cw_sb[:, k], op=mybir.AluOpType.mult)

        def store(v, k0, k1):
            rows = out[TILES * v : TILES * (v + 1)].rearrange("r (q c) l -> q r (c l)", c=TILES)
            nc.sync.dma_start(out=rows[:, :, L * k0 : L * k1], in_=res[v][:, k0:k1].rearrange("p c l -> p (c l)"))

        def finish(v, i0, i1):
            for i in range(i0, i1):
                c = order[v][i]
                weigh(v, c)
                k = CLASS_OF_TILE[c]
                if v == 0 and i < 2:
                    store(v, k, k + 1)
                elif i % 2 == 1:
                    store(v, k - 1, k + 1)

        deal_a(vcopy, slice(1, 3), 0)
        deal_a(scopy, slice(0, 4, 3), 2)
        deal_shared(0)
        quantise(a_mx, a_bf[:])
        for n in range(1, SLOTS):
            deal_shared(n)
            first(n - 1)
        turn(0, 0)
        quantise(x_mx[3], x_bf[3][:])
        turn(0, 1)
        passes(3)
        nc.gpsimd.tensor_scalar(
            out=b_bf[:, 0:HALF],
            in0=b_raw[:].rearrange("p t l -> p l t")[:, 0:HALF],
            scalar1=1.0,
            scalar2=0.0,
            op0=mybir.AluOpType.mult,
            op1=mybir.AluOpType.add,
        )
        scopy(
            out=b_bf[:, HALF:].rearrange("p (n i) u -> p n u i", i=PACK),
            in_=b_raw[:, :, HALF:].rearrange("p u (n i) -> p n u i", i=PACK),
        )
        round_z(scopy, 0, 0, 8)
        turn(1, 0)
        turn(1, 1)
        round_z(scopy, 1, 0, 8)
        turn(2, 0)
        turn(2, 1)
        round_z(scopy, 2, 0, 8)
        turn(3, 0)
        turn(3, 1)
        round_z(scopy, 3, 0, 4)
        quantise(b_mx, b_bf[:].unsqueeze(1))
        quantise(z_mx[0], z_bf[0][:])
        second(0, order[0])
        round_z(vcopy, 3, 4, 8)
        quantise(z_mx[1], z_bf[1][:])
        finish(0, 0, 2)
        second(1, order[1])
        finish(0, 2, 4)
        finish(1, 0, 4)
